import numpy as np
import ml_dtypes


def mxq(x, axis, fmt="e4m3"):
    dtype, down = {"e4m3": (ml_dtypes.float8_e4m3fn, 7), "e5m2": (ml_dtypes.float8_e5m2, 14)}[fmt]
    v = np.moveaxis(np.asarray(x, np.float32).astype(ml_dtypes.bfloat16).astype(np.float64), axis, -1)
    blocks = v.reshape(v.shape[:-1] + (-1, 32))
    amax = np.abs(blocks).max(-1, keepdims=True)
    byte = np.maximum(np.where(amax > 0, np.frexp(amax)[1] - 1 + 127, 0) - down, 1)
    scale = np.exp2(byte - 127.0)
    codes = (blocks / scale).astype(np.float32).astype(dtype).astype(np.float64)
    return np.moveaxis((codes * scale).reshape(v.shape), -1, axis)


WIDE = False


def mx_kscale(k):
    if not WIDE:
        return np.ones(k)
    levels = np.array([10, -10, 5, -5, 0])
    if k % 512:
        return np.exp2(np.random.permutation(np.resize(levels, k // 32))).repeat(32)
    a = np.empty((k // 512, 16))
    for p in range(k // 512):
        a[p, :8] = np.random.permutation(np.resize(levels, 8))
        for g in range(8):
            far = levels[np.abs(levels - a[p, g]) >= 10]
            a[p, g + 8] = far[np.random.randint(len(far))]
    return np.exp2(a.ravel()).repeat(32)


def f64(x):
    return np.asarray(x).astype(np.float64)


def striped(idx):
    return np.tile(idx.reshape(-1, 16).T, (8, 1)).astype(np.uint16)


def unstriped(offs):
    return offs[:16].T.reshape(-1).astype(np.int64)


def silu(v):
    return v / (1.0 + np.exp(-np.maximum(v, -700.0)))


K, T, S, N = 1536, 2048, 1280, 128


def setup_inputs():
    n = np.random.standard_normal
    s = mx_kscale(K)[:, None]
    return {
        "xT": (n((K, T)) * s).astype(np.float32),
        "w": (n((K, N)) / np.sqrt(K) / s).astype(np.float32),
        "b": (0.3 * n((N, 1))).astype(np.float32),
        "offs": striped(np.random.permutation(T)[:S]),
    }


def reference(xT, w, b, offs):
    idx = unstriped(offs)
    xq = mxq(f64(xT)[:, idx], 0, "e4m3")
    y = mxq(f64(w), 0, "e4m3").T @ xq
    y = silu(y + f64(b))
    return y

@@ -1,0 +1,170 @@
+from contextlib import ExitStack
+
+import concourse.mybir as mybir
+
+K, T, S, N = 1536, 2048, 1280, 128
+FLOPS = 2 * K * S * N
+
+F32 = mybir.dt.float32
+BF16 = mybir.dt.bfloat16
+U32 = mybir.dt.uint32
+U16 = mybir.dt.uint16
+U8 = mybir.dt.uint8
+FP8X4 = mybir.dt.float8_e4m3fn_x4
+COPY = mybir.ActivationFunctionType.Copy
+SILU = mybir.ActivationFunctionType.Silu
+
+P = 128
+PACK = 4
+K_PASS = P * PACK
+PASSES = K // K_PASS
+LIST_ROWS = 16
+RUN = 4
+QUANT_TOKENS = 512
+
+CHUNKS = (((512, 384),) * 4, ((512, 384),) * 4, ((512, 384), (512, 384), (512, 256), (256, 128), (256, 128)))
+OUT_SLICES = (512, 512, 256)
+EARLY_SLICES = (512, 512, 256)
+BYTE_SLICES = (512, 768)
+
+
+def cuts(widths):
+    out = []
+    at = 0
+    for width in widths:
+        out.append((at, at + width))
+        at += width
+    return out
+
+
+def interleave_views(grouped, raw, lo, hi):
+    dst = grouped[:, lo:hi, :].rearrange("p (c i) j -> p c j i", i=RUN)
+    src = raw[:, :, lo:hi].rearrange("p j (c i) -> p c j i", i=RUN)
+    return dst, src
+
+
+def tile_picked_pick_lin_silu_sub_e_kernel(tc, xT, w, b, offs, out):
+    nc = tc.nc
+    with ExitStack() as ctx:
+        keep = ctx.enter_context(tc.tile_pool(name="keep", bufs=1))
+        psum = ctx.enter_context(tc.psum_pool(name="psum", bufs=1))
+
+        offsets = keep.tile([P, S // LIST_ROWS], U16, name="offsets")
+        bias = keep.tile([P, 1], F32, name="bias")
+        zero = keep.tile([P, 1], F32, name="zero")
+        warm = keep.tile([P, 1], F32, name="warm")
+        x_scales = keep.tile([P, T], U8, name="x_scales", align_bytes=64)
+        x_words = [keep.tile([P, T], U32, name="x_words%d" % a, align_bytes=64) for a in range(PASSES)]
+
+        raws = {}
+        for a in range(PASSES):
+            rows = xT[a * K_PASS : (a + 1) * K_PASS, :].rearrange("(p j) t -> p j t", j=PACK)
+            for c, (lo, hi) in enumerate(cuts([width for width, share in CHUNKS[a]])):
+                raw = keep.tile([P, PACK, hi - lo], F32, name="raw%d_%d" % (a, c), align_bytes=64)
+                nc.sync.dma_start(out=raw[:], in_=rows[:, :, lo:hi])
+                raws[a, c] = raw
+                if (a, c) == (0, 0):
+                    nc.sync.dma_start(offsets[:], offs)
+        w_raw = []
+        for a in range(PASSES):
+            tile = keep.tile([P, PACK, N], F32, name="w_raw%d" % a, align_bytes=64)
+            nc.sync.dma_start(out=tile[:], in_=w[a * K_PASS : (a + 1) * K_PASS, :].rearrange("(p j) n -> p j n", j=PACK))
+            w_raw.append(tile)
+        nc.sync.dma_start(out=bias[:], in_=b)
+
+        nc.vector.memset(zero[:], 0.0)
+        nc.scalar.activation(out=warm[:], in_=zero[:], func=SILU, bias=zero[:])
+        nc.gpsimd.memset(x_scales[:], 0)
+
+        def picked(window, lo, hi):
+            return window[:].indirect(offsets[:, lo // LIST_ROWS : hi // LIST_ROWS])
+
+        got_words = {}
+
+        def gather_words(a, lo, hi):
+            got = keep.tile([P, hi - lo], U32, name="got_words%d_%d" % (a, lo), align_bytes=64)
+            nc.vector.tensor_copy(got[:], picked(x_words[a], lo, hi))
+            got_words[a, lo] = got
+
+        def words_of(a, lo, hi):
+            start = max(s for (aa, s) in got_words if aa == a and s <= lo)
+            return got_words[a, start][:, lo - start : hi - start]
+
+        pending = []
+        for a in range(PASSES):
+            for c, (lo, hi) in enumerate(cuts([width for width, share in CHUNKS[a]])):
+                width, share = CHUNKS[a][c]
+                grouped = keep.tile([P, width, PACK], BF16, name="grouped%d_%d" % (a, c), align_bytes=64)
+                if share > 0:
+                    dst, src = interleave_views(grouped, raws[a, c], 0, share)
+                    nc.scalar.activation(out=dst, in_=src, func=COPY)
+                if share < width:
+                    dst, src = interleave_views(grouped, raws[a, c], share, width)
+                    nc.vector.tensor_copy(out=dst, in_=src)
+                if pending:
+                    gather_words(*pending.pop(0))
+                for q0 in range(0, width, QUANT_TOKENS):
+                    q1 = min(width, q0 + QUANT_TOKENS)
+                    nc.vector.quantize_mx(
+                        out=x_words[a][:, lo + q0 : lo + q1].bitcast(FP8X4),
+                        scales=x_scales[PACK * a : P, lo + q0 : lo + q1],
+                        in_=grouped[:, q0:q1, :].rearrange("p t j -> p (t j)"),
+                    )
+            if a < PASSES - 1:
+                pending.extend((a, lo, hi) for lo, hi in cuts(EARLY_SLICES))
+        assert not pending
+
+        w_words, w_scales = [], []
+
+        def quantize_w(a):
+            grouped = keep.tile([P, N, PACK], BF16, name="w_grouped%d" % a, align_bytes=64)
+            dst, src = interleave_views(grouped, w_raw[a], 0, N)
+            nc.scalar.activation(out=dst, in_=src, func=COPY)
+            words = keep.tile([P, N], U32, name="w_words%d" % a, align_bytes=64)
+            scales = keep.tile([P, N], U8, name="w_scales%d" % a, align_bytes=64)
+            nc.vector.quantize_mx(
+                out=words[:].bitcast(FP8X4), scales=scales[:], in_=grouped[:].rearrange("p n j -> p (n j)")
+            )
+            w_words.append(words)
+            w_scales.append(scales)
+
+        got_scales = {}
+
+        def gather_scales(lo, hi):
+            got = keep.tile([P, hi - lo], U8, name="got_scales%d" % lo, align_bytes=64)
+            nc.vector.tensor_copy(got[:], picked(x_scales, lo, hi))
+            got_scales[lo] = got
+
+        banks = {}
+
+        def multiply(a, lo, hi):
+            if a == 0:
+                banks[lo] = psum.tile([N, hi - lo], F32, name="bank%d" % lo)
+            start = max(s for s in got_scales if s <= lo)
+            nc.tensor.matmul_mx(
+                out=banks[lo][:],
+                lhsT=w_words[a][:].bitcast(FP8X4),
+                lhsT_scale=w_scales[a][:],
+                rhs=words_of(a, lo, hi).bitcast(FP8X4),
+                rhs_scale=got_scales[start][PACK * a : P, lo - start : hi - start],
+                start=(a == 0),
+                stop=(a == PASSES - 1),
+            )
+
+        last = PASSES - 1
+        for n, (blo, bhi) in enumerate(cuts(BYTE_SLICES)):
+            gather_scales(blo, bhi)
+            if n == 0:
+                for a in range(last):
+                    quantize_w(a)
+            for lo, hi in cuts(OUT_SLICES):
+                if blo <= lo < bhi:
+                    for a in range(last):
+                        multiply(a, lo, hi)
+        quantize_w(last)
+        for lo, hi in cuts(OUT_SLICES):
+            gather_words(last, lo, hi)
+            multiply(last, lo, hi)
+            y = keep.tile([N, hi - lo], F32, name="y%d" % lo)
+            nc.scalar.activation(out=y[:], in_=banks[lo][:], func=SILU, bias=bias[:])
+            nc.sync.dma_start(out=out[:, lo:hi], in_=y[:])

@@ -18,29 +18,35 @@ P = 128
 PACK = 4
 K_PASS = P * PACK
 PASSES = K // K_PASS
+LAST = PASSES - 1
 LIST_ROWS = 16
 RUN = 4
-QUANT_TOKENS = 512
 
-CHUNKS = (((512, 384),) * 4, ((512, 384),) * 4, ((512, 384), (512, 384), (512, 256), (256, 128), (256, 128)))
-OUT_SLICES = (512, 512, 256)
-EARLY_SLICES = (512, 512, 256)
-BYTE_SLICES = (512, 768)
+STAGES = ((1024, 1024), (1024, 1024), (512, 512, 512, 256, 256))
+STEPS = (
+    ((512, 0), (512, 512), (512, 0), (512, 512)),
+    ((512, 256), (512, 512), (512, 0), (512, 512)),
+    ((512, 512), (512, 384), (512, 256), (256, 256), (256, 128)),
+)
+EARLY_GATHERS = (512, 512, 256)
+OUT_SLICES = (512, 256, 256, 256)
+FIRST_SCALES = 768
 
 
 def cuts(widths):
-    out = []
-    at = 0
+    spans = []
+    start = 0
     for width in widths:
-        out.append((at, at + width))
-        at += width
-    return out
+        spans.append((start, start + width))
+        start += width
+    return spans
 
 
-def interleave_views(grouped, raw, lo, hi):
-    dst = grouped[:, lo:hi, :].rearrange("p (c i) j -> p c j i", i=RUN)
-    src = raw[:, :, lo:hi].rearrange("p j (c i) -> p c j i", i=RUN)
-    return dst, src
+def interleaved(grouped, raw):
+    return (
+        grouped.rearrange("p (c i) j -> p c j i", i=RUN),
+        raw.rearrange("p j (c i) -> p c j i", i=RUN),
+    )
 
 
 def tile_picked_pick_lin_silu_sub_e_kernel(tc, xT, w, b, offs, out):
@@ -49,122 +55,110 @@ def tile_picked_pick_lin_silu_sub_e_kernel(tc, xT, w, b, offs, out):
         keep = ctx.enter_context(tc.tile_pool(name="keep", bufs=1))
         psum = ctx.enter_context(tc.psum_pool(name="psum", bufs=1))
 
-        offsets = keep.tile([P, S // LIST_ROWS], U16, name="offsets")
-        bias = keep.tile([P, 1], F32, name="bias")
-        zero = keep.tile([P, 1], F32, name="zero")
-        warm = keep.tile([P, 1], F32, name="warm")
-        x_scales = keep.tile([P, T], U8, name="x_scales", align_bytes=64)
-        x_words = [keep.tile([P, T], U32, name="x_words%d" % a, align_bytes=64) for a in range(PASSES)]
+        def by_partition(rows, a):
+            return rows[a * K_PASS : (a + 1) * K_PASS, :].rearrange("(p j) c -> p j c", j=PACK)
 
-        raws = {}
+        offsets = keep.tile([P, S // LIST_ROWS], U16, name="offsets")
+        x_raw = {}
         for a in range(PASSES):
-            rows = xT[a * K_PASS : (a + 1) * K_PASS, :].rearrange("(p j) t -> p j t", j=PACK)
-            for c, (lo, hi) in enumerate(cuts([width for width, share in CHUNKS[a]])):
-                raw = keep.tile([P, PACK, hi - lo], F32, name="raw%d_%d" % (a, c), align_bytes=64)
+            rows = by_partition(xT, a)
+            for lo, hi in cuts(STAGES[a]):
+                raw = keep.tile([P, PACK, hi - lo], F32, name="x_raw%d_%d" % (a, lo), align_bytes=64)
+                x_raw[a, lo] = raw
                 nc.sync.dma_start(out=raw[:], in_=rows[:, :, lo:hi])
-                raws[a, c] = raw
-                if (a, c) == (0, 0):
+                if (a, lo) == (0, 0):
                     nc.sync.dma_start(offsets[:], offs)
         w_raw = []
         for a in range(PASSES):
-            tile = keep.tile([P, PACK, N], F32, name="w_raw%d" % a, align_bytes=64)
-            nc.sync.dma_start(out=tile[:], in_=w[a * K_PASS : (a + 1) * K_PASS, :].rearrange("(p j) n -> p j n", j=PACK))
-            w_raw.append(tile)
+            raw = keep.tile([P, PACK, N], F32, name="w_raw%d" % a, tag="w_raw%d" % a, align_bytes=64)
+            nc.sync.dma_start(out=raw[:], in_=by_partition(w, a))
+            w_raw.append(raw)
+        bias = keep.tile([P, 1], F32, name="bias")
         nc.sync.dma_start(out=bias[:], in_=b)
 
+        zero = keep.tile([P, 1], F32, name="zero")
+        unused = keep.tile([P, 1], F32, name="unused")
         nc.vector.memset(zero[:], 0.0)
-        nc.scalar.activation(out=warm[:], in_=zero[:], func=SILU, bias=zero[:])
+        nc.scalar.activation(out=unused[:], in_=zero[:], func=SILU, bias=zero[:])
+
+        x_scales = keep.tile([P, T], U8, name="x_scales", align_bytes=64)
         nc.gpsimd.memset(x_scales[:], 0)
+        x_words = [keep.tile([P, T], U32, name="x_words%d" % a, align_bytes=64) for a in range(PASSES)]
 
-        def picked(window, lo, hi):
-            return window[:].indirect(offsets[:, lo // LIST_ROWS : hi // LIST_ROWS])
+        def gather(dst, window, lo, hi):
+            nc.vector.tensor_copy(dst, window[:].indirect(offsets[:, lo // LIST_ROWS : hi // LIST_ROWS]))
 
-        got_words = {}
-
-        def gather_words(a, lo, hi):
-            got = keep.tile([P, hi - lo], U32, name="got_words%d_%d" % (a, lo), align_bytes=64)
-            nc.vector.tensor_copy(got[:], picked(x_words[a], lo, hi))
-            got_words[a, lo] = got
-
-        def words_of(a, lo, hi):
-            start = max(s for (aa, s) in got_words if aa == a and s <= lo)
-            return got_words[a, start][:, lo - start : hi - start]
-
-        pending = []
+        picked_words = [keep.tile([P, S], U32, name="picked_words%d" % a, align_bytes=64) for a in range(LAST)]
+        waiting = []
         for a in range(PASSES):
-            for c, (lo, hi) in enumerate(cuts([width for width, share in CHUNKS[a]])):
-                width, share = CHUNKS[a][c]
-                grouped = keep.tile([P, width, PACK], BF16, name="grouped%d_%d" % (a, c), align_bytes=64)
+            for step, (lo, hi) in enumerate(cuts([width for width, share in STEPS[a]])):
+                width, share = STEPS[a][step]
+                stage = max(start for start, stop in cuts(STAGES[a]) if start <= lo)
+                raw = x_raw[a, stage][:, :, lo - stage : hi - stage]
+                grouped = keep.tile([P, width, PACK], BF16, name="x_grouped%d_%d" % (a, lo), align_bytes=64)
                 if share > 0:
-                    dst, src = interleave_views(grouped, raws[a, c], 0, share)
+                    dst, src = interleaved(grouped[:, :share, :], raw[:, :, :share])
                     nc.scalar.activation(out=dst, in_=src, func=COPY)
                 if share < width:
-                    dst, src = interleave_views(grouped, raws[a, c], share, width)
+                    dst, src = interleaved(grouped[:, share:, :], raw[:, :, share:])
                     nc.vector.tensor_copy(out=dst, in_=src)
-                if pending:
-                    gather_words(*pending.pop(0))
-                for q0 in range(0, width, QUANT_TOKENS):
-                    q1 = min(width, q0 + QUANT_TOKENS)
-                    nc.vector.quantize_mx(
-                        out=x_words[a][:, lo + q0 : lo + q1].bitcast(FP8X4),
-                        scales=x_scales[PACK * a : P, lo + q0 : lo + q1],
-                        in_=grouped[:, q0:q1, :].rearrange("p t j -> p (t j)"),
-                    )
-            if a < PASSES - 1:
-                pending.extend((a, lo, hi) for lo, hi in cuts(EARLY_SLICES))
-        assert not pending
+                if waiting:
+                    g0, g1 = waiting.pop(0)
+                    gather(picked_words[a - 1][:, g0:g1], x_words[a - 1], g0, g1)
+                nc.vector.quantize_mx(
+                    out=x_words[a][:, lo:hi].bitcast(FP8X4),
+                    scales=x_scales[PACK * a :, lo:hi],
+                    in_=grouped[:].rearrange("p t j -> p (t j)"),
+                )
+            waiting = cuts(EARLY_GATHERS)
 
-        w_words, w_scales = [], []
-
-        def quantize_w(a):
-            grouped = keep.tile([P, N, PACK], BF16, name="w_grouped%d" % a, align_bytes=64)
-            dst, src = interleave_views(grouped, w_raw[a], 0, N)
-            nc.scalar.activation(out=dst, in_=src, func=COPY)
-            words = keep.tile([P, N], U32, name="w_words%d" % a, align_bytes=64)
-            scales = keep.tile([P, N], U8, name="w_scales%d" % a, align_bytes=64)
+        def quantize_w(passes, tag):
+            count = len(passes)
+            grouped = keep.tile([P, count, N, PACK], BF16, name=tag + "_grouped", align_bytes=64)
+            for n, a in enumerate(passes):
+                dst, src = interleaved(grouped[:, n, :, :], w_raw[a][:])
+                nc.scalar.activation(out=dst, in_=src, func=COPY)
+            words = keep.tile([P, count * N], U32, name=tag + "_words", align_bytes=64)
+            scales = keep.tile([P, count * N], U8, name=tag + "_scales", align_bytes=64)
             nc.vector.quantize_mx(
-                out=words[:].bitcast(FP8X4), scales=scales[:], in_=grouped[:].rearrange("p n j -> p (n j)")
+                out=words[:].bitcast(FP8X4),
+                scales=scales[:],
+                in_=grouped[:].rearrange("p a n j -> p (a n j)"),
             )
-            w_words.append(words)
-            w_scales.append(scales)
+            return [(words[:, n * N : (n + 1) * N], scales[:, n * N : (n + 1) * N]) for n in range(count)]
 
-        got_scales = {}
+        first_scales = keep.tile([P, FIRST_SCALES], U8, name="first_scales", align_bytes=64)
+        gather(first_scales[:], x_scales, 0, FIRST_SCALES)
+        weights = quantize_w(list(range(LAST)), "w_early") + quantize_w([LAST], "w_last")
+        other_scales = keep.tile([P, S - FIRST_SCALES], U8, name="other_scales", tag="w_raw%d" % (LAST - 1), align_bytes=64)
+        gather(other_scales[:], x_scales, FIRST_SCALES, S)
+        last_words = keep.tile([P, S], U32, name="last_words", tag="w_raw%d" % LAST, align_bytes=64)
+        picked_words.append(last_words)
 
-        def gather_scales(lo, hi):
-            got = keep.tile([P, hi - lo], U8, name="got_scales%d" % lo, align_bytes=64)
-            nc.vector.tensor_copy(got[:], picked(x_scales, lo, hi))
-            got_scales[lo] = got
+        banks = [psum.tile([N, hi - lo], F32, name="bank%d" % lo) for lo, hi in cuts(OUT_SLICES)]
 
-        banks = {}
-
-        def multiply(a, lo, hi):
-            if a == 0:
-                banks[lo] = psum.tile([N, hi - lo], F32, name="bank%d" % lo)
-            start = max(s for s in got_scales if s <= lo)
+        def multiply(a, bank, lo, hi):
+            if lo < FIRST_SCALES:
+                scales = first_scales[PACK * a :, lo:hi]
+            else:
+                scales = other_scales[PACK * a :, lo - FIRST_SCALES : hi - FIRST_SCALES]
+            w_words, w_scales = weights[a]
             nc.tensor.matmul_mx(
-                out=banks[lo][:],
-                lhsT=w_words[a][:].bitcast(FP8X4),
-                lhsT_scale=w_scales[a][:],
-                rhs=words_of(a, lo, hi).bitcast(FP8X4),
-                rhs_scale=got_scales[start][PACK * a : P, lo - start : hi - start],
+                out=bank[:],
+                lhsT=w_words.bitcast(FP8X4),
+                lhsT_scale=w_scales,
+                rhs=picked_words[a][:, lo:hi].bitcast(FP8X4),
+                rhs_scale=scales,
                 start=(a == 0),
-                stop=(a == PASSES - 1),
+                stop=(a == LAST),
             )
 
-        last = PASSES - 1
-        for n, (blo, bhi) in enumerate(cuts(BYTE_SLICES)):
-            gather_scales(blo, bhi)
-            if n == 0:
-                for a in range(last):
-                    quantize_w(a)
-            for lo, hi in cuts(OUT_SLICES):
-                if blo <= lo < bhi:
-                    for a in range(last):
-                        multiply(a, lo, hi)
-        quantize_w(last)
-        for lo, hi in cuts(OUT_SLICES):
-            gather_words(last, lo, hi)
-            multiply(last, lo, hi)
+        for bank, (lo, hi) in zip(banks, cuts(OUT_SLICES)):
+            for a in range(LAST):
+                multiply(a, bank, lo, hi)
+        for bank, (lo, hi) in zip(banks, cuts(OUT_SLICES)):
+            gather(last_words[:, lo:hi], x_words[LAST], lo, hi)
+            multiply(LAST, bank, lo, hi)
             y = keep.tile([N, hi - lo], F32, name="y%d" % lo)
-            nc.scalar.activation(out=y[:], in_=banks[lo][:], func=SILU, bias=bias[:])
+            nc.scalar.activation(out=y[:], in_=bank[:], func=SILU, bias=bias[:])
             nc.sync.dma_start(out=out[:, lo:hi], in_=y[:])

@@ -7,6 +7,7 @@ FLOPS = 2 * K * S * N
 
 F32 = mybir.dt.float32
 BF16 = mybir.dt.bfloat16
+I32 = mybir.dt.int32
 U32 = mybir.dt.uint32
 U16 = mybir.dt.uint16
 U8 = mybir.dt.uint8
@@ -22,15 +23,19 @@ LAST = PASSES - 1
 LIST_ROWS = 16
 RUN = 4
 
-STAGES = ((1024, 1024), (1024, 1024), (512, 512, 512, 256, 256))
-STEPS = (
-    ((512, 0), (512, 512), (512, 0), (512, 512)),
-    ((512, 256), (512, 512), (512, 0), (512, 512)),
-    ((512, 512), (512, 384), (512, 256), (256, 256), (256, 128)),
+LOADS = (
+    ((2048, 704),),
+    ((1024, 1024), (1024, 384)),
+    ((1024, 1024), (1024, 1024)),
+    ((1024, 1024), (1024, 640)),
+    ((1024, 1024), (1024, 1024)),
+    ((1024, 1024), (512, 512), (512, 192)),
 )
-EARLY_GATHERS = (512, 512, 256)
-OUT_SLICES = (512, 256, 256, 256)
-FIRST_SCALES = 768
+SLICES = (512, 256, 256, 256)
+EARLY = (1024, 256)
+W_AFTER = {(1, 1024): (0,), (5, 1536): (1, 2)}
+HOLDS = {(2, 0): "w_raw2"}
+WEAVERS = ("vv", "vv", "sssv")
 
 
 def cuts(widths):
@@ -42,17 +47,11 @@ def cuts(widths):
     return spans
 
 
-def interleaved(grouped, raw):
-    return (
-        grouped.rearrange("p (c i) j -> p c j i", i=RUN),
-        raw.rearrange("p j (c i) -> p c j i", i=RUN),
-    )
-
-
 def tile_picked_pick_lin_silu_sub_e_kernel(tc, xT, w, b, offs, out):
     nc = tc.nc
     with ExitStack() as ctx:
         keep = ctx.enter_context(tc.tile_pool(name="keep", bufs=1))
+        ring = ctx.enter_context(tc.tile_pool(name="ring", bufs=4))
         psum = ctx.enter_context(tc.psum_pool(name="psum", bufs=1))
 
         def by_partition(rows, a):
@@ -60,20 +59,25 @@ def tile_picked_pick_lin_silu_sub_e_kernel(tc, xT, w, b, offs, out):
 
         offsets = keep.tile([P, S // LIST_ROWS], U16, name="offsets")
         x_raw = {}
-        for a in range(PASSES):
-            rows = by_partition(xT, a)
-            for lo, hi in cuts(STAGES[a]):
-                raw = keep.tile([P, PACK, hi - lo], F32, name="x_raw%d_%d" % (a, lo), align_bytes=64)
-                x_raw[a, lo] = raw
-                nc.sync.dma_start(out=raw[:], in_=rows[:, :, lo:hi])
-                if (a, lo) == (0, 0):
-                    nc.sync.dma_start(offsets[:], offs)
-        w_raw = []
-        for a in range(PASSES):
-            raw = keep.tile([P, PACK, N], F32, name="w_raw%d" % a, tag="w_raw%d" % a, align_bytes=64)
-            nc.sync.dma_start(out=raw[:], in_=by_partition(w, a))
-            w_raw.append(raw)
+        w_raw = {}
         bias = keep.tile([P, 1], F32, name="bias")
+
+        def load_w(passes):
+            for a in passes:
+                raw = keep.tile([P, PACK, N], F32, name="w_raw%d" % a, tag="w_raw%d" % a, align_bytes=64)
+                nc.sync.dma_start(out=raw[:], in_=by_partition(w, a))
+                w_raw[a] = raw
+
+        for q in range(2 * PASSES):
+            a, u = divmod(q, 2)
+            rows = by_partition(xT, a)[:, 2 * u : 2 * u + 2, :]
+            for lo, hi in cuts([width for width, share in LOADS[q]]):
+                raw = keep.tile([P, 2, hi - lo], F32, name="x_raw%d_%d" % (q, lo), tag="x_raw%d_%d" % (q, lo), align_bytes=64)
+                x_raw[q, lo] = raw
+                nc.sync.dma_start(out=raw[:], in_=rows[:, :, lo:hi])
+                if (q, lo) == (0, 0):
+                    nc.sync.dma_start(offsets[:], offs)
+                load_w(W_AFTER.get((q, lo), ()))
         nc.sync.dma_start(out=bias[:], in_=b)
 
         zero = keep.tile([P, 1], F32, name="zero")
@@ -81,43 +85,73 @@ def tile_picked_pick_lin_silu_sub_e_kernel(tc, xT, w, b, offs, out):
         nc.vector.memset(zero[:], 0.0)
         nc.scalar.activation(out=unused[:], in_=zero[:], func=SILU, bias=zero[:])
 
-        x_scales = keep.tile([P, T], U8, name="x_scales", align_bytes=64)
-        nc.gpsimd.memset(x_scales[:], 0)
-        x_words = [keep.tile([P, T], U32, name="x_words%d" % a, align_bytes=64) for a in range(PASSES)]
+        spans = cuts(SLICES)
+        pieces = [cuts(EARLY)] * LAST + [spans]
+        picked = {}
+        codes = {}
 
-        def gather(dst, window, lo, hi):
-            nc.vector.tensor_copy(dst, window[:].indirect(offsets[:, lo // LIST_ROWS : hi // LIST_ROWS]))
-
-        picked_words = [keep.tile([P, S], U32, name="picked_words%d" % a, align_bytes=64) for a in range(LAST)]
-        waiting = []
-        for a in range(PASSES):
-            for step, (lo, hi) in enumerate(cuts([width for width, share in STEPS[a]])):
-                width, share = STEPS[a][step]
-                stage = max(start for start, stop in cuts(STAGES[a]) if start <= lo)
-                raw = x_raw[a, stage][:, :, lo - stage : hi - stage]
-                grouped = keep.tile([P, width, PACK], BF16, name="x_grouped%d_%d" % (a, lo), align_bytes=64)
+        def round_pair(q):
+            pairs = ring.tile([P, T], U32, name="pairs")
+            for (lo, hi), (width, share) in zip(cuts([wd for wd, sh in LOADS[q]]), LOADS[q]):
+                raw = x_raw[q, lo]
                 if share > 0:
-                    dst, src = interleaved(grouped[:, :share, :], raw[:, :, :share])
-                    nc.scalar.activation(out=dst, in_=src, func=COPY)
+                    nc.scalar.activation(
+                        out=pairs[:, lo : lo + share].bitcast(BF16).rearrange("p (t j) -> p t j", j=2),
+                        in_=raw[:, :, :share].rearrange("p j t -> p t j"),
+                        func=COPY,
+                    )
                 if share < width:
-                    dst, src = interleaved(grouped[:, share:, :], raw[:, :, share:])
-                    nc.vector.tensor_copy(out=dst, in_=src)
-                if waiting:
-                    g0, g1 = waiting.pop(0)
-                    gather(picked_words[a - 1][:, g0:g1], x_words[a - 1], g0, g1)
-                nc.vector.quantize_mx(
-                    out=x_words[a][:, lo:hi].bitcast(FP8X4),
-                    scales=x_scales[PACK * a :, lo:hi],
-                    in_=grouped[:].rearrange("p t j -> p (t j)"),
-                )
-            waiting = cuts(EARLY_GATHERS)
+                    nc.vector.tensor_copy(
+                        out=pairs[:, lo + share : hi].bitcast(BF16).rearrange("p (t j) -> p t j", j=2),
+                        in_=raw[:, :, share:].rearrange("p j t -> p t j"),
+                    )
+                if q < 2 * PASSES - 1 and (q, lo) in W_AFTER:
+                    quantize_w(W_AFTER[q, lo], "w%d" % q)
+            return pairs
+
+        def gather(q, pairs, s):
+            a, u = divmod(q, 2)
+            lo, hi = pieces[a][s]
+            if u == 0:
+                picked[a, s] = keep.tile([P, 2, hi - lo], U32, name="picked%d_%d" % (a, s), align_bytes=64)
+            nc.vector.tensor_copy(
+                picked[a, s][:, u, :], pairs[:].indirect(offsets[:, lo // LIST_ROWS : hi // LIST_ROWS])
+            )
+
+        woven = {}
+
+        def weave(a, s):
+            lo, hi = pieces[a][s]
+            tile = keep.tile([P, hi - lo, 2], U32, name="woven%d_%d" % (a, s), tag=HOLDS.get((a, s), "woven%d_%d" % (a, s)), align_bytes=64)
+            src = picked[a, s][:].rearrange("p u n -> p n u")
+            if WEAVERS[a][s] == "s":
+                nc.scalar.copy(out=tile[:], in_=src)
+            else:
+                nc.vector.tensor_copy(out=tile[:].bitcast(I32), in_=src.bitcast(I32))
+            woven[a, s] = tile
+
+        def quantize(a, s):
+            lo, hi = pieces[a][s]
+            words = keep.tile([P, hi - lo], U32, name="words%d_%d" % (a, s), align_bytes=64)
+            scales = keep.tile([P, hi - lo], U8, name="scales%d_%d" % (a, s), align_bytes=64)
+            nc.vector.quantize_mx(
+                out=words[:].bitcast(FP8X4),
+                scales=scales[:],
+                in_=woven[a, s][:].rearrange("p n u -> p (n u)").bitcast(BF16),
+            )
+            codes[a, s] = (words, scales)
+
+        weights = {}
 
         def quantize_w(passes, tag):
             count = len(passes)
             grouped = keep.tile([P, count, N, PACK], BF16, name=tag + "_grouped", align_bytes=64)
             for n, a in enumerate(passes):
-                dst, src = interleaved(grouped[:, n, :, :], w_raw[a][:])
-                nc.scalar.activation(out=dst, in_=src, func=COPY)
+                nc.scalar.activation(
+                    out=grouped[:, n, :, :].rearrange("p (c i) j -> p c j i", i=RUN),
+                    in_=w_raw[a][:].rearrange("p j (c i) -> p c j i", i=RUN),
+                    func=COPY,
+                )
             words = keep.tile([P, count * N], U32, name=tag + "_words", align_bytes=64)
             scales = keep.tile([P, count * N], U8, name=tag + "_scales", align_bytes=64)
             nc.vector.quantize_mx(
@@ -125,40 +159,56 @@ def tile_picked_pick_lin_silu_sub_e_kernel(tc, xT, w, b, offs, out):
                 scales=scales[:],
                 in_=grouped[:].rearrange("p a n j -> p (a n j)"),
             )
-            return [(words[:, n * N : (n + 1) * N], scales[:, n * N : (n + 1) * N]) for n in range(count)]
+            for n, a in enumerate(passes):
+                weights[a] = (words[:, n * N : (n + 1) * N], scales[:, n * N : (n + 1) * N])
 
-        first_scales = keep.tile([P, FIRST_SCALES], U8, name="first_scales", align_bytes=64)
-        gather(first_scales[:], x_scales, 0, FIRST_SCALES)
-        weights = quantize_w(list(range(LAST)), "w_early") + quantize_w([LAST], "w_last")
-        other_scales = keep.tile([P, S - FIRST_SCALES], U8, name="other_scales", tag="w_raw%d" % (LAST - 1), align_bytes=64)
-        gather(other_scales[:], x_scales, FIRST_SCALES, S)
-        last_words = keep.tile([P, S], U32, name="last_words", tag="w_raw%d" % LAST, align_bytes=64)
-        picked_words.append(last_words)
+        banks = [psum.tile([N, hi - lo], F32, name="bank%d" % lo) for lo, hi in spans]
 
-        banks = [psum.tile([N, hi - lo], F32, name="bank%d" % lo) for lo, hi in cuts(OUT_SLICES)]
-
-        def multiply(a, bank, lo, hi):
-            if lo < FIRST_SCALES:
-                scales = first_scales[PACK * a :, lo:hi]
-            else:
-                scales = other_scales[PACK * a :, lo - FIRST_SCALES : hi - FIRST_SCALES]
+        def multiply(a, s):
             w_words, w_scales = weights[a]
+            lo, hi = spans[s]
+            n = max(i for i, (start, stop) in enumerate(pieces[a]) if start <= lo)
+            first = pieces[a][n][0]
+            words, scales = codes[a, n]
             nc.tensor.matmul_mx(
-                out=bank[:],
+                out=banks[s][:],
                 lhsT=w_words.bitcast(FP8X4),
                 lhsT_scale=w_scales,
-                rhs=picked_words[a][:, lo:hi].bitcast(FP8X4),
-                rhs_scale=scales,
+                rhs=words[:, lo - first : hi - first].bitcast(FP8X4),
+                rhs_scale=scales[:, lo - first : hi - first],
                 start=(a == 0),
                 stop=(a == LAST),
             )
 
-        for bank, (lo, hi) in zip(banks, cuts(OUT_SLICES)):
-            for a in range(LAST):
-                multiply(a, bank, lo, hi)
-        for bank, (lo, hi) in zip(banks, cuts(OUT_SLICES)):
-            gather(last_words[:, lo:hi], x_words[LAST], lo, hi)
-            multiply(LAST, bank, lo, hi)
+        def finish(s):
+            lo, hi = spans[s]
             y = keep.tile([N, hi - lo], F32, name="y%d" % lo)
-            nc.scalar.activation(out=y[:], in_=bank[:], func=SILU, bias=bias[:])
+            nc.scalar.activation(out=y[:], in_=banks[s][:], func=SILU, bias=bias[:])
             nc.sync.dma_start(out=out[:, lo:hi], in_=y[:])
+
+        count = len(SLICES)
+        for q in range(2 * PASSES - 1):
+            a, u = divmod(q, 2)
+            pairs = round_pair(q)
+            for s in range(len(pieces[a])):
+                gather(q, pairs, s)
+            if u == 1:
+                for s in range(len(EARLY)):
+                    weave(a, s)
+                for s in range(len(EARLY)):
+                    quantize(a, s)
+        pairs = round_pair(2 * PASSES - 1)
+        for s in range(count):
+            multiply(0, s)
+        gather(2 * PASSES - 1, pairs, 0)
+        gather(2 * PASSES - 1, pairs, 1)
+        quantize_w([1, 2], "w_late")
+        for s in range(count):
+            multiply(1, s)
+        for s in range(count):
+            if 0 < s < count - 1:
+                gather(2 * PASSES - 1, pairs, s + 1)
+            weave(LAST, s)
+            quantize(LAST, s)
+            multiply(LAST, s)
+            finish(s)

@@ -14,6 +14,8 @@ U8 = mybir.dt.uint8
 FP8X4 = mybir.dt.float8_e4m3fn_x4
 COPY = mybir.ActivationFunctionType.Copy
 SILU = mybir.ActivationFunctionType.Silu
+MULT = mybir.AluOpType.mult
+ADD = mybir.AluOpType.add
 
 P = 128
 PACK = 4
@@ -24,18 +26,20 @@ LIST_ROWS = 16
 RUN = 4
 
 LOADS = (
-    ((2048, 704),),
-    ((1024, 1024), (1024, 384)),
-    ((1024, 1024), (1024, 1024)),
-    ((1024, 1024), (1024, 640)),
-    ((1024, 1024), (1024, 1024)),
-    ((1024, 1024), (512, 512), (512, 192)),
+    ((2048, 704, 0),),
+    ((1024, 1024, 0), (1024, 384, 0)),
+    ((1024, 512, 512), (1024, 1024, 0)),
+    ((1024, 1024, 0), (1024, 576, 448)),
+    ((1024, 512, 512), (1024, 512, 0)),
+    ((1024, 384, 640), (1024, 832, 192)),
 )
-SLICES = (512, 256, 256, 256)
-EARLY = (1024, 256)
-W_AFTER = {(1, 1024): (0,), (5, 1536): (1, 2)}
-HOLDS = {(2, 0): "w_raw2"}
-WEAVERS = ("vv", "vv", "sssv")
+SLICES = (512, 512, 256)
+EARLY = (512, 768)
+W_AFTER = {(5, 1024): (0, 1, 2)}
+HOLDS = {(2, 0): "w_raw2", (1, 0): "x_raw4_0", (1, 1): "x_raw4_1024"}
+QUANTIZE_WIDTHS = {256: (256,), 512: (512,), 768: (512, 256), 1024: (1024,), 1280: (1024, 256)}
+UNITS = (512, 256, 256, 256)
+WEAVERS = ("sv", "ss", "sss")
 
 
 def cuts(widths):
@@ -71,7 +75,7 @@ def tile_picked_pick_lin_silu_sub_e_kernel(tc, xT, w, b, offs, out):
         for q in range(2 * PASSES):
             a, u = divmod(q, 2)
             rows = by_partition(xT, a)[:, 2 * u : 2 * u + 2, :]
-            for lo, hi in cuts([width for width, share in LOADS[q]]):
+            for lo, hi in cuts([width for width, share, pool in LOADS[q]]):
                 raw = keep.tile([P, 2, hi - lo], F32, name="x_raw%d_%d" % (q, lo), tag="x_raw%d_%d" % (q, lo), align_bytes=64)
                 x_raw[q, lo] = raw
                 nc.sync.dma_start(out=raw[:], in_=rows[:, :, lo:hi])
@@ -90,32 +94,38 @@ def tile_picked_pick_lin_silu_sub_e_kernel(tc, xT, w, b, offs, out):
         picked = {}
         codes = {}
 
+        def round_on(engine, dst, src):
+            if engine == "s":
+                nc.scalar.activation(out=dst, in_=src, func=COPY)
+            elif engine == "v":
+                nc.vector.tensor_copy(out=dst, in_=src)
+            else:
+                nc.gpsimd.tensor_scalar(out=dst, in0=src, scalar1=1.0, scalar2=0.0, op0=MULT, op1=ADD)
+
         def round_pair(q):
             pairs = ring.tile([P, T], U32, name="pairs")
-            for (lo, hi), (width, share) in zip(cuts([wd for wd, sh in LOADS[q]]), LOADS[q]):
+            for (lo, hi), (width, share, pool) in zip(cuts([load[0] for load in LOADS[q]]), LOADS[q]):
                 raw = x_raw[q, lo]
-                if share > 0:
-                    nc.scalar.activation(
-                        out=pairs[:, lo : lo + share].bitcast(BF16).rearrange("p (t j) -> p t j", j=2),
-                        in_=raw[:, :, :share].rearrange("p j t -> p t j"),
-                        func=COPY,
-                    )
-                if share < width:
-                    nc.vector.tensor_copy(
-                        out=pairs[:, lo + share : hi].bitcast(BF16).rearrange("p (t j) -> p t j", j=2),
-                        in_=raw[:, :, share:].rearrange("p j t -> p t j"),
-                    )
-                if q < 2 * PASSES - 1 and (q, lo) in W_AFTER:
-                    quantize_w(W_AFTER[q, lo], "w%d" % q)
+                for engine, (c0, c1) in zip("sgv", cuts([share, pool, width - share - pool])):
+                    if c1 > c0:
+                        round_on(
+                            engine,
+                            pairs[:, lo + c0 : lo + c1].bitcast(BF16).rearrange("p (t j) -> p t j", j=2),
+                            raw[:, :, c0:c1].rearrange("p j t -> p t j"),
+                        )
+                if q < 2 * PASSES - 1:
+                    for a in W_AFTER.get((q, lo), ()):
+                        grouped = keep.tile([P, N * PACK], BF16, name="w_grouped%d" % a, align_bytes=64)
+                        quantize_w((a,), "s", grouped[:])
             return pairs
 
-        def gather(q, pairs, s):
+        for a in range(PASSES):
+            picked[a] = keep.tile([P, 2, S], U32, name="picked%d" % a, align_bytes=64)
+
+        def gather(q, pairs, lo, hi):
             a, u = divmod(q, 2)
-            lo, hi = pieces[a][s]
-            if u == 0:
-                picked[a, s] = keep.tile([P, 2, hi - lo], U32, name="picked%d_%d" % (a, s), align_bytes=64)
             nc.vector.tensor_copy(
-                picked[a, s][:, u, :], pairs[:].indirect(offsets[:, lo // LIST_ROWS : hi // LIST_ROWS])
+                picked[a][:, u, lo:hi], pairs[:].indirect(offsets[:, lo // LIST_ROWS : hi // LIST_ROWS])
             )
 
         woven = {}
@@ -123,65 +133,64 @@ def tile_picked_pick_lin_silu_sub_e_kernel(tc, xT, w, b, offs, out):
         def weave(a, s):
             lo, hi = pieces[a][s]
             tile = keep.tile([P, hi - lo, 2], U32, name="woven%d_%d" % (a, s), tag=HOLDS.get((a, s), "woven%d_%d" % (a, s)), align_bytes=64)
-            src = picked[a, s][:].rearrange("p u n -> p n u")
+            src = picked[a][:, :, lo:hi].rearrange("p u n -> p n u")
             if WEAVERS[a][s] == "s":
                 nc.scalar.copy(out=tile[:], in_=src)
             else:
                 nc.vector.tensor_copy(out=tile[:].bitcast(I32), in_=src.bitcast(I32))
             woven[a, s] = tile
 
+        for a in range(PASSES):
+            codes[a] = (
+                keep.tile([P, S], U32, name="words%d" % a, align_bytes=64),
+                keep.tile([P, S], U8, name="scales%d" % a, align_bytes=64),
+            )
+
         def quantize(a, s):
             lo, hi = pieces[a][s]
-            words = keep.tile([P, hi - lo], U32, name="words%d_%d" % (a, s), align_bytes=64)
-            scales = keep.tile([P, hi - lo], U8, name="scales%d_%d" % (a, s), align_bytes=64)
-            nc.vector.quantize_mx(
-                out=words[:].bitcast(FP8X4),
-                scales=scales[:],
-                in_=woven[a, s][:].rearrange("p n u -> p (n u)").bitcast(BF16),
-            )
-            codes[a, s] = (words, scales)
+            words, scales = codes[a]
+            for c0, c1 in cuts(QUANTIZE_WIDTHS[hi - lo]):
+                nc.vector.quantize_mx(
+                    out=words[:, lo + c0 : lo + c1].bitcast(FP8X4),
+                    scales=scales[:, lo + c0 : lo + c1],
+                    in_=woven[a, s][:, c0:c1, :].rearrange("p n u -> p (n u)").bitcast(BF16),
+                )
 
         weights = {}
 
-        def quantize_w(passes, tag):
+        def quantize_w(passes, engine, grouped):
             count = len(passes)
-            grouped = keep.tile([P, count, N, PACK], BF16, name=tag + "_grouped", align_bytes=64)
             for n, a in enumerate(passes):
-                nc.scalar.activation(
-                    out=grouped[:, n, :, :].rearrange("p (c i) j -> p c j i", i=RUN),
-                    in_=w_raw[a][:].rearrange("p j (c i) -> p c j i", i=RUN),
-                    func=COPY,
+                round_on(
+                    engine,
+                    grouped[:, n * K_PASS : (n + 1) * K_PASS].rearrange("p (c i j) -> p c j i", i=RUN, j=PACK),
+                    w_raw[a][:].rearrange("p j (c i) -> p c j i", i=RUN),
                 )
-            words = keep.tile([P, count * N], U32, name=tag + "_words", align_bytes=64)
-            scales = keep.tile([P, count * N], U8, name=tag + "_scales", align_bytes=64)
-            nc.vector.quantize_mx(
-                out=words[:].bitcast(FP8X4),
-                scales=scales[:],
-                in_=grouped[:].rearrange("p a n j -> p (a n j)"),
-            )
+            words = keep.tile([P, count * N], U32, name="w_words%d" % passes[0], align_bytes=64)
+            scales = keep.tile([P, count * N], U8, name="w_scales%d" % passes[0], align_bytes=64)
+            nc.vector.quantize_mx(out=words[:].bitcast(FP8X4), scales=scales[:], in_=grouped)
             for n, a in enumerate(passes):
                 weights[a] = (words[:, n * N : (n + 1) * N], scales[:, n * N : (n + 1) * N])
 
-        banks = [psum.tile([N, hi - lo], F32, name="bank%d" % lo) for lo, hi in spans]
+        units = cuts(UNITS)
+        banks = [psum.tile([N, hi - lo], F32, name="bank%d" % lo) for lo, hi in units]
 
         def multiply(a, s):
             w_words, w_scales = weights[a]
-            lo, hi = spans[s]
-            n = max(i for i, (start, stop) in enumerate(pieces[a]) if start <= lo)
-            first = pieces[a][n][0]
-            words, scales = codes[a, n]
+            lo, hi = units[s]
+            words, scales = codes[a]
             nc.tensor.matmul_mx(
                 out=banks[s][:],
                 lhsT=w_words.bitcast(FP8X4),
                 lhsT_scale=w_scales,
-                rhs=words[:, lo - first : hi - first].bitcast(FP8X4),
-                rhs_scale=scales[:, lo - first : hi - first],
+                rhs=words[:, lo:hi].bitcast(FP8X4),
+                rhs_scale=scales[:, lo:hi],
                 start=(a == 0),
                 stop=(a == LAST),
             )
 
         def finish(s):
-            lo, hi = spans[s]
+            lo, hi = units[s]
             y = keep.tile([N, hi - lo], F32, name="y%d" % lo)
             nc.scalar.activation(out=y[:], in_=banks[s][:], func=SILU, bias=bias[:])
             nc.sync.dma_start(out=out[:, lo:hi], in_=y[:])
@@ -190,25 +199,33 @@ def tile_picked_pick_lin_silu_sub_e_kernel(tc, xT, w, b, offs, out):
         for q in range(2 * PASSES - 1):
             a, u = divmod(q, 2)
             pairs = round_pair(q)
-            for s in range(len(pieces[a])):
-                gather(q, pairs, s)
-            if u == 1:
+            if u == 0:
+                gather(q, pairs, 0, S)
+            else:
+                for lo, hi in pieces[a]:
+                    gather(q, pairs, lo, hi)
                 for s in range(len(EARLY)):
                     weave(a, s)
                 for s in range(len(EARLY)):
                     quantize(a, s)
         pairs = round_pair(2 * PASSES - 1)
+        late = {512: (0, 1), 1024: (2,)}
+        for a in range(LAST):
+            if a in weights:
+                for s in range(len(units)):
+                    multiply(a, s)
+        for lo, hi in cuts(SLICES):
+            if lo in late:
+                quantize_w(late[lo], "s", picked[LAST][:, 1, lo : lo + 2 * N * len(late[lo])].bitcast(BF16))
+                for a in late[lo]:
+                    if a < LAST:
+                        for s in range(len(units)):
+                            multiply(a, s)
+            gather(2 * PASSES - 1, pairs, lo, hi)
         for s in range(count):
-            multiply(0, s)
-        gather(2 * PASSES - 1, pairs, 0)
-        gather(2 * PASSES - 1, pairs, 1)
-        quantize_w([1, 2], "w_late")
-        for s in range(count):
-            multiply(1, s)
-        for s in range(count):
-            if 0 < s < count - 1:
-                gather(2 * PASSES - 1, pairs, s + 1)
             weave(LAST, s)
             quantize(LAST, s)
-            multiply(LAST, s)
-            finish(s)
+            for r, (lo, hi) in enumerate(units):
+                if spans[s][0] <= lo < spans[s][1]:
+                    multiply(LAST, r)
+                    finish(r)

@@ -22,24 +22,28 @@ PACK = 4
 K_PASS = P * PACK
 PASSES = K // K_PASS
 LAST = PASSES - 1
+PAIRS = 2 * PASSES
+LAST_PAIR = PAIRS - 1
 LIST_ROWS = 16
 RUN = 4
+HALF = T // 2
+QUARTER = T // 4
 
+WITH_FREE_VECTOR = 352
+WITH_EQUAL_HELPER = 576
+WHILE_WEAVING = 320
 LOADS = (
-    ((2048, 704, 0),),
-    ((1024, 1024, 0), (1024, 384, 0)),
-    ((1024, 512, 512), (1024, 1024, 0)),
-    ((1024, 1024, 0), (1024, 576, 448)),
-    ((1024, 512, 512), (1024, 512, 0)),
-    ((1024, 384, 640), (1024, 832, 192)),
+    ((T, 2 * WITH_FREE_VECTOR, "vector"),),
+    ((HALF, HALF, None), (HALF, WITH_FREE_VECTOR, "vector")),
+    ((HALF, WITH_EQUAL_HELPER, "gpsimd"), (HALF, HALF, None)),
+    ((HALF, HALF, None), (HALF, WITH_EQUAL_HELPER, "gpsimd")),
+    ((HALF, WITH_EQUAL_HELPER, "gpsimd"), (HALF, WITH_EQUAL_HELPER, "vector")),
+    ((HALF, WHILE_WEAVING, "gpsimd"), (QUARTER, QUARTER // 2, "gpsimd"), (QUARTER, QUARTER, None)),
 )
-SLICES = (512, 512, 256)
-EARLY = (512, 768)
-W_AFTER = {(5, 1024): (0, 1, 2)}
-HOLDS = {(2, 0): "w_raw2", (1, 0): "x_raw4_0", (1, 1): "x_raw4_1024"}
-QUANTIZE_WIDTHS = {256: (256,), 512: (512,), 768: (512, 256), 1024: (1024,), 1280: (1024, 256)}
-UNITS = (512, 256, 256, 256)
-WEAVERS = ("sv", "ss", "sss")
+EARLY_PIECES = (512, 768)
+LAST_PIECES = (512, 512, 256)
+QUANTIZE_WIDTHS = {256: (256,), 512: (512,), 768: (512, 256)}
+OUT_SLICES = (512, 256, 256, 256)
 
 
 def cuts(widths):
@@ -56,32 +60,37 @@ def tile_picked_pick_lin_silu_sub_e_kernel(tc, xT, w, b, offs, out):
     with ExitStack() as ctx:
         keep = ctx.enter_context(tc.tile_pool(name="keep", bufs=1))
         ring = ctx.enter_context(tc.tile_pool(name="ring", bufs=4))
+        shared = ctx.enter_context(tc.tile_pool(name="shared", bufs=1))
         psum = ctx.enter_context(tc.psum_pool(name="psum", bufs=1))
 
         def by_partition(rows, a):
             return rows[a * K_PASS : (a + 1) * K_PASS, :].rearrange("(p j) c -> p j c", j=PACK)
 
+        first_load_of_pair_4 = "x_raw4_0"
+        last_load_of_w = "w_raw%d" % LAST
+        woven_bytes = EARLY_PIECES[1] * PACK * 2
+
         offsets = keep.tile([P, S // LIST_ROWS], U16, name="offsets")
         x_raw = {}
-        w_raw = {}
-        bias = keep.tile([P, 1], F32, name="bias")
-
-        def load_w(passes):
-            for a in passes:
-                raw = keep.tile([P, PACK, N], F32, name="w_raw%d" % a, tag="w_raw%d" % a, align_bytes=64)
-                nc.sync.dma_start(out=raw[:], in_=by_partition(w, a))
-                w_raw[a] = raw
-
-        for q in range(2 * PASSES):
+        for q in range(PAIRS):
             a, u = divmod(q, 2)
             rows = by_partition(xT, a)[:, 2 * u : 2 * u + 2, :]
-            for lo, hi in cuts([width for width, share, pool in LOADS[q]]):
-                raw = keep.tile([P, 2, hi - lo], F32, name="x_raw%d_%d" % (q, lo), tag="x_raw%d_%d" % (q, lo), align_bytes=64)
+            for lo, hi in cuts([load[0] for load in LOADS[q]]):
+                if (q, lo) == (LAST_PAIR - 1, HALF):
+                    raw = shared.tile([P, 2, hi - lo], F32, name="x_raw_shared", offset=0, align_bytes=64)
+                else:
+                    name = "x_raw%d_%d" % (q, lo)
+                    raw = keep.tile([P, 2, hi - lo], F32, name=name, tag=name, align_bytes=64)
                 x_raw[q, lo] = raw
                 nc.sync.dma_start(out=raw[:], in_=rows[:, :, lo:hi])
                 if (q, lo) == (0, 0):
                     nc.sync.dma_start(offsets[:], offs)
-                load_w(W_AFTER.get((q, lo), ()))
+        w_raw = []
+        for a in range(PASSES):
+            raw = keep.tile([P, PACK, N], F32, name="w_raw%d" % a, tag="w_raw%d" % a, align_bytes=64)
+            nc.sync.dma_start(out=raw[:], in_=by_partition(w, a))
+            w_raw.append(raw)
+        bias = keep.tile([P, 1], F32, name="bias")
         nc.sync.dma_start(out=bias[:], in_=b)
 
         zero = keep.tile([P, 1], F32, name="zero")
@@ -89,82 +98,76 @@ def tile_picked_pick_lin_silu_sub_e_kernel(tc, xT, w, b, offs, out):
         nc.vector.memset(zero[:], 0.0)
         nc.scalar.activation(out=unused[:], in_=zero[:], func=SILU, bias=zero[:])
 
-        spans = cuts(SLICES)
-        pieces = [cuts(EARLY)] * LAST + [spans]
-        picked = {}
-        codes = {}
-
-        def round_on(engine, dst, src):
-            if engine == "s":
-                nc.scalar.activation(out=dst, in_=src, func=COPY)
-            elif engine == "v":
-                nc.vector.tensor_copy(out=dst, in_=src)
-            else:
-                nc.gpsimd.tensor_scalar(out=dst, in0=src, scalar1=1.0, scalar2=0.0, op0=MULT, op1=ADD)
+        pieces = [cuts(EARLY_PIECES)] * LAST + [cuts(LAST_PIECES)]
+        out_spans = cuts(OUT_SLICES)
 
         def round_pair(q):
-            pairs = ring.tile([P, T], U32, name="pairs")
-            for (lo, hi), (width, share, pool) in zip(cuts([load[0] for load in LOADS[q]]), LOADS[q]):
-                raw = x_raw[q, lo]
-                for engine, (c0, c1) in zip("sgv", cuts([share, pool, width - share - pool])):
-                    if c1 > c0:
-                        round_on(
-                            engine,
-                            pairs[:, lo + c0 : lo + c1].bitcast(BF16).rearrange("p (t j) -> p t j", j=2),
-                            raw[:, :, c0:c1].rearrange("p j t -> p t j"),
-                        )
-                if q < 2 * PASSES - 1:
-                    for a in W_AFTER.get((q, lo), ()):
-                        grouped = keep.tile([P, N * PACK], BF16, name="w_grouped%d" % a, align_bytes=64)
-                        quantize_w((a,), "s", grouped[:])
-            return pairs
+            if q == LAST_PAIR:
+                window = shared.tile([P, T], U32, name="window_shared", offset=woven_bytes, align_bytes=64)
+            else:
+                window = ring.tile([P, T], U32, name="window")
+            for (lo, hi), (width, share, helper) in zip(cuts([load[0] for load in LOADS[q]]), LOADS[q]):
+                dst = window[:, lo:hi].bitcast(BF16).rearrange("p (t j) -> p t j", j=2)
+                src = x_raw[q, lo][:].rearrange("p j t -> p t j")
+                nc.scalar.activation(out=dst[:, :share, :], in_=src[:, :share, :], func=COPY)
+                if helper == "vector":
+                    nc.vector.tensor_copy(out=dst[:, share:, :], in_=src[:, share:, :])
+                if helper == "gpsimd":
+                    nc.gpsimd.tensor_scalar(
+                        out=dst[:, share:, :], in0=src[:, share:, :], scalar1=1.0, scalar2=0.0, op0=MULT, op1=ADD
+                    )
+            return window
 
-        for a in range(PASSES):
-            picked[a] = keep.tile([P, 2, S], U32, name="picked%d" % a, align_bytes=64)
+        picked = {}
+        for a in range(LAST):
+            whole = keep.tile([P, 2, S], U32, name="picked%d" % a, align_bytes=64)
+            picked[a, 0, S] = whole[:]
+            for lo, hi in pieces[a]:
+                picked[a, lo, hi] = whole[:, :, lo:hi]
+        for lo, hi in pieces[LAST]:
+            picked[LAST, lo, hi] = keep.tile([P, 2, hi - lo], U32, name="picked_last%d" % lo, align_bytes=64)[:]
 
-        def gather(q, pairs, lo, hi):
+        def gather(q, window, lo, hi):
             a, u = divmod(q, 2)
             nc.vector.tensor_copy(
-                picked[a][:, u, lo:hi], pairs[:].indirect(offsets[:, lo // LIST_ROWS : hi // LIST_ROWS])
+                picked[a, lo, hi][:, u, :], window[:].indirect(offsets[:, lo // LIST_ROWS : hi // LIST_ROWS])
             )
 
-        woven = {}
-
-        def weave(a, s):
-            lo, hi = pieces[a][s]
-            tile = keep.tile([P, hi - lo, 2], U32, name="woven%d_%d" % (a, s), tag=HOLDS.get((a, s), "woven%d_%d" % (a, s)), align_bytes=64)
-            src = picked[a][:, :, lo:hi].rearrange("p u n -> p n u")
-            if WEAVERS[a][s] == "s":
-                nc.scalar.copy(out=tile[:], in_=src)
+        def weave(a, lo, hi):
+            shape = [P, hi - lo, 2]
+            name = "woven%d_%d" % (a, lo)
+            if a == LAST - 1 and lo > 0:
+                woven = shared.tile(shape, U32, name=name, offset=0, align_bytes=64)
             else:
-                nc.vector.tensor_copy(out=tile[:].bitcast(I32), in_=src.bitcast(I32))
-            woven[a, s] = tile
+                tag = {(0, 0): "x_raw2_0", (1, 0): first_load_of_pair_4, (LAST, 0): last_load_of_w}.get((a, lo), name)
+                woven = keep.tile(shape, U32, name=name, tag=tag, align_bytes=64)
+            src = picked[a, lo, hi].rearrange("p u n -> p n u")
+            if a == 0 and lo > 0:
+                nc.vector.tensor_copy(out=woven[:].bitcast(I32), in_=src.bitcast(I32))
+            else:
+                nc.scalar.copy(out=woven[:], in_=src)
+            return woven
 
-        for a in range(PASSES):
-            codes[a] = (
-                keep.tile([P, S], U32, name="words%d" % a, align_bytes=64),
-                keep.tile([P, S], U8, name="scales%d" % a, align_bytes=64),
-            )
+        x_words = [keep.tile([P, S], U32, name="x_words%d" % a, align_bytes=64) for a in range(PASSES)]
+        x_scales = [keep.tile([P, S], U8, name="x_scales%d" % a, align_bytes=64) for a in range(PASSES)]
 
-        def quantize(a, s):
-            lo, hi = pieces[a][s]
-            words, scales = codes[a]
+        def quantize(a, lo, hi, woven):
             for c0, c1 in cuts(QUANTIZE_WIDTHS[hi - lo]):
                 nc.vector.quantize_mx(
-                    out=words[:, lo + c0 : lo + c1].bitcast(FP8X4),
-                    scales=scales[:, lo + c0 : lo + c1],
-                    in_=woven[a, s][:, c0:c1, :].rearrange("p n u -> p (n u)").bitcast(BF16),
+                    out=x_words[a][:, lo + c0 : lo + c1].bitcast(FP8X4),
+                    scales=x_scales[a][:, lo + c0 : lo + c1],
+                    in_=woven[:, c0:c1, :].rearrange("p n u -> p (n u)").bitcast(BF16),
                 )
 
         weights = {}
 
-        def quantize_w(passes, engine, grouped):
+        def quantize_w(passes, grouped):
             count = len(passes)
             for n, a in enumerate(passes):
-                round_on(
-                    engine,
-                    grouped[:, n * K_PASS : (n + 1) * K_PASS].rearrange("p (c i j) -> p c j i", i=RUN, j=PACK),
-                    w_raw[a][:].rearrange("p j (c i) -> p c j i", i=RUN),
+                nc.scalar.activation(
+                    out=grouped[:, n * K_PASS : (n + 1) * K_PASS].rearrange("p (c i j) -> p c j i", i=RUN, j=PACK),
+                    in_=w_raw[a][:].rearrange("p j (c i) -> p c j i", i=RUN),
+                    func=COPY,
                 )
             words = keep.tile([P, count * N], U32, name="w_words%d" % passes[0], align_bytes=64)
             scales = keep.tile([P, count * N], U8, name="w_scales%d" % passes[0], align_bytes=64)
@@ -172,60 +175,45 @@ def tile_picked_pick_lin_silu_sub_e_kernel(tc, xT, w, b, offs, out):
             for n, a in enumerate(passes):
                 weights[a] = (words[:, n * N : (n + 1) * N], scales[:, n * N : (n + 1) * N])
 
-        units = cuts(UNITS)
-        banks = [psum.tile([N, hi - lo], F32, name="bank%d" % lo) for lo, hi in units]
+        banks = [psum.tile([N, hi - lo], F32, name="bank%d" % lo) for lo, hi in out_spans]
 
-        def multiply(a, s):
+        def multiply(a, bank, lo, hi):
             w_words, w_scales = weights[a]
-            lo, hi = units[s]
-            words, scales = codes[a]
             nc.tensor.matmul_mx(
-                out=banks[s][:],
+                out=bank[:],
                 lhsT=w_words.bitcast(FP8X4),
                 lhsT_scale=w_scales,
-                rhs=words[:, lo:hi].bitcast(FP8X4),
-                rhs_scale=scales[:, lo:hi],
+                rhs=x_words[a][:, lo:hi].bitcast(FP8X4),
+                rhs_scale=x_scales[a][:, lo:hi],
                 start=(a == 0),
                 stop=(a == LAST),
             )
 
-        def finish(s):
-            lo, hi = units[s]
-            y = keep.tile([N, hi - lo], F32, name="y%d" % lo)
-            nc.scalar.activation(out=y[:], in_=banks[s][:], func=SILU, bias=bias[:])
-            nc.sync.dma_start(out=out[:, lo:hi], in_=y[:])
-
-        count = len(SLICES)
-        for q in range(2 * PASSES - 1):
+        for q in range(LAST_PAIR):
             a, u = divmod(q, 2)
-            pairs = round_pair(q)
-            if u == 0:
-                gather(q, pairs, 0, S)
-            else:
-                for lo, hi in pieces[a]:
-                    gather(q, pairs, lo, hi)
-                for s in range(len(EARLY)):
-                    weave(a, s)
-                for s in range(len(EARLY)):
-                    quantize(a, s)
-        pairs = round_pair(2 * PASSES - 1)
-        late = {512: (0, 1), 1024: (2,)}
+            window = round_pair(q)
+            for lo, hi in [(0, S)] if u == 0 and a < LAST else pieces[a]:
+                gather(q, window, lo, hi)
+            if u == 1:
+                woven = [weave(a, lo, hi) for lo, hi in pieces[a]]
+                for (lo, hi), tile in zip(pieces[a], woven):
+                    quantize(a, lo, hi, tile)
+
+        window = round_pair(LAST_PAIR)
+        first, second, third = pieces[LAST]
+        gather(LAST_PAIR, window, *first)
+        quantize_w(list(range(LAST)), picked[(LAST,) + second][:, 1, :].bitcast(BF16))
         for a in range(LAST):
-            if a in weights:
-                for s in range(len(units)):
-                    multiply(a, s)
-        for lo, hi in cuts(SLICES):
-            if lo in late:
-                quantize_w(late[lo], "s", picked[LAST][:, 1, lo : lo + 2 * N * len(late[lo])].bitcast(BF16))
-                for a in late[lo]:
-                    if a < LAST:
-                        for s in range(len(units)):
-                            multiply(a, s)
-            gather(2 * PASSES - 1, pairs, lo, hi)
-        for s in range(count):
-            weave(LAST, s)
-            quantize(LAST, s)
-            for r, (lo, hi) in enumerate(units):
-                if spans[s][0] <= lo < spans[s][1]:
-                    multiply(LAST, r)
-                    finish(r)
+            for bank, (lo, hi) in zip(banks, out_spans):
+                multiply(a, bank, lo, hi)
+        gather(LAST_PAIR, window, *second)
+        quantize_w([LAST], picked[(LAST,) + third][:, 1, :].bitcast(BF16))
+        gather(LAST_PAIR, window, *third)
+        for start, stop in pieces[LAST]:
+            quantize(LAST, start, stop, weave(LAST, start, stop))
+            for bank, (lo, hi) in zip(banks, out_spans):
+                if start <= lo < stop:
+                    multiply(LAST, bank, lo, hi)
+                    y = keep.tile([N, hi - lo], F32, name="y%d" % lo)
+                    nc.scalar.activation(out=y[:], in_=bank[:], func=SILU, bias=bias[:])
+                    nc.sync.dma_start(out=out[:, lo:hi], in_=y[:])

@@ -29,15 +29,15 @@ RUN = 4
 HALF = T // 2
 QUARTER = T // 4
 
-WITH_FREE_VECTOR = 352
-WITH_EQUAL_HELPER = 576
-WHILE_WEAVING = 320
-LOADS = (
-    ((T, 2 * WITH_FREE_VECTOR, "vector"),),
-    ((HALF, HALF, None), (HALF, WITH_FREE_VECTOR, "vector")),
-    ((HALF, WITH_EQUAL_HELPER, "gpsimd"), (HALF, HALF, None)),
-    ((HALF, HALF, None), (HALF, WITH_EQUAL_HELPER, "gpsimd")),
-    ((HALF, WITH_EQUAL_HELPER, "gpsimd"), (HALF, WITH_EQUAL_HELPER, "vector")),
+WITH_VECTOR = 352
+WITH_GPSIMD = 576
+WHILE_WEAVING = 416
+STEPS = (
+    ((T, 2 * WITH_VECTOR, "vector"),),
+    ((HALF, WITH_GPSIMD, "gpsimd"), (HALF, WITH_VECTOR, "vector")),
+    ((HALF, WITH_GPSIMD, "gpsimd"), (HALF, HALF, None)),
+    ((HALF, WITH_GPSIMD, "gpsimd"), (HALF, WITH_GPSIMD, "gpsimd")),
+    ((HALF, WITH_GPSIMD, "gpsimd"), (HALF, WITH_VECTOR, "vector")),
     ((HALF, WHILE_WEAVING, "gpsimd"), (QUARTER, QUARTER // 2, "gpsimd"), (QUARTER, QUARTER, None)),
 )
 EARLY_PIECES = (512, 768)
@@ -66,25 +66,29 @@ def tile_picked_pick_lin_silu_sub_e_kernel(tc, xT, w, b, offs, out):
         def by_partition(rows, a):
             return rows[a * K_PASS : (a + 1) * K_PASS, :].rearrange("(p j) c -> p j c", j=PACK)
 
-        first_load_of_pair_4 = "x_raw4_0"
         last_load_of_w = "w_raw%d" % LAST
         woven_bytes = EARLY_PIECES[1] * PACK * 2
 
         offsets = keep.tile([P, S // LIST_ROWS], U16, name="offsets")
+        pair_rows = xT.rearrange("(a p u e) t -> a u p (e t)", p=P, u=2, e=2)
         x_raw = {}
-        for q in range(PAIRS):
+        for q in range(LAST_PAIR):
             a, u = divmod(q, 2)
-            rows = by_partition(xT, a)[:, 2 * u : 2 * u + 2, :]
-            for lo, hi in cuts([load[0] for load in LOADS[q]]):
-                if (q, lo) == (LAST_PAIR - 1, HALF):
-                    raw = shared.tile([P, 2, hi - lo], F32, name="x_raw_shared", offset=0, align_bytes=64)
-                else:
-                    name = "x_raw%d_%d" % (q, lo)
-                    raw = keep.tile([P, 2, hi - lo], F32, name=name, tag=name, align_bytes=64)
-                x_raw[q, lo] = raw
-                nc.sync.dma_start(out=raw[:], in_=rows[:, :, lo:hi])
-                if (q, lo) == (0, 0):
-                    nc.sync.dma_start(offsets[:], offs)
+            if q == LAST_PAIR - 1:
+                raw = shared.tile([P, 2 * T], F32, name="x_raw_shared", offset=0, align_bytes=64)
+            else:
+                raw = keep.tile([P, 2 * T], F32, name="x_raw%d" % q, align_bytes=64)
+            start = 0
+            for lo, hi in cuts([step[0] for step in STEPS[q]]):
+                nc.sync.dma_start(out=raw[:, start : T + hi], in_=pair_rows[a, u][:, start : T + hi])
+                x_raw[q, lo] = raw[:].rearrange("p (e t) -> p e t", e=2)[:, :, lo:hi]
+                start = T + hi
+            if q == 0:
+                nc.sync.dma_start(offsets[:], offs)
+        for lo, hi in cuts([step[0] for step in STEPS[LAST_PAIR]]):
+            raw = keep.tile([P, 2, hi - lo], F32, name="x_last%d" % lo, align_bytes=64)
+            nc.sync.dma_start(out=raw[:], in_=by_partition(xT, LAST)[:, 2:, lo:hi])
+            x_raw[LAST_PAIR, lo] = raw[:]
         w_raw = []
         for a in range(PASSES):
             raw = keep.tile([P, PACK, N], F32, name="w_raw%d" % a, tag="w_raw%d" % a, align_bytes=64)
@@ -106,9 +110,9 @@ def tile_picked_pick_lin_silu_sub_e_kernel(tc, xT, w, b, offs, out):
                 window = shared.tile([P, T], U32, name="window_shared", offset=woven_bytes, align_bytes=64)
             else:
                 window = ring.tile([P, T], U32, name="window")
-            for (lo, hi), (width, share, helper) in zip(cuts([load[0] for load in LOADS[q]]), LOADS[q]):
+            for (lo, hi), (width, share, helper) in zip(cuts([step[0] for step in STEPS[q]]), STEPS[q]):
                 dst = window[:, lo:hi].bitcast(BF16).rearrange("p (t j) -> p t j", j=2)
-                src = x_raw[q, lo][:].rearrange("p j t -> p t j")
+                src = x_raw[q, lo].rearrange("p j t -> p t j")
                 nc.scalar.activation(out=dst[:, :share, :], in_=src[:, :share, :], func=COPY)
                 if helper == "vector":
                     nc.vector.tensor_copy(out=dst[:, share:, :], in_=src[:, share:, :])
@@ -139,7 +143,7 @@ def tile_picked_pick_lin_silu_sub_e_kernel(tc, xT, w, b, offs, out):
             if a == LAST - 1 and lo > 0:
                 woven = shared.tile(shape, U32, name=name, offset=0, align_bytes=64)
             else:
-                tag = {(0, 0): "x_raw2_0", (1, 0): first_load_of_pair_4, (LAST, 0): last_load_of_w}.get((a, lo), name)
+                tag = last_load_of_w if (a, lo) == (LAST, 0) else name
                 woven = keep.tile(shape, U32, name=name, tag=tag, align_bytes=64)
             src = picked[a, lo, hi].rearrange("p u n -> p n u")
             if a == 0 and lo > 0:

@@ -41,7 +41,7 @@ STEPS = (
     ((HALF, WHILE_WEAVING, "gpsimd"), (QUARTER, QUARTER // 2, "gpsimd"), (QUARTER, QUARTER, None)),
 )
 EARLY_PIECES = (512, 768)
-LAST_PIECES = (512, 512, 256)
+LAST_PIECES = (512, 256, 256, 256)
 QUANTIZE_WIDTHS = {256: (256,), 512: (512,), 768: (512, 256)}
 OUT_SLICES = (512, 256, 256, 256)
 
@@ -66,7 +66,7 @@ def tile_picked_pick_lin_silu_sub_e_kernel(tc, xT, w, b, offs, out):
         def by_partition(rows, a):
             return rows[a * K_PASS : (a + 1) * K_PASS, :].rearrange("(p j) c -> p j c", j=PACK)
 
-        last_load_of_w = "w_raw%d" % LAST
+        last_load_of_w = "w_raw0"
         woven_bytes = EARLY_PIECES[1] * PACK * 2
 
         offsets = keep.tile([P, S // LIST_ROWS], U16, name="offsets")
@@ -89,10 +89,15 @@ def tile_picked_pick_lin_silu_sub_e_kernel(tc, xT, w, b, offs, out):
             raw = keep.tile([P, 2, hi - lo], F32, name="x_last%d" % lo, align_bytes=64)
             nc.sync.dma_start(out=raw[:], in_=by_partition(xT, LAST)[:, 2:, lo:hi])
             x_raw[LAST_PAIR, lo] = raw[:]
+        held = keep.tile([P, S + PASSES * K_PASS], F32, name="held", align_bytes=64)
         w_raw = []
         for a in range(PASSES):
-            raw = keep.tile([P, PACK, N], F32, name="w_raw%d" % a, tag="w_raw%d" % a, align_bytes=64)
-            nc.sync.dma_start(out=raw[:], in_=by_partition(w, a))
+            if a == 0:
+                raw = keep.tile([P, PACK, N], F32, name="w_raw0", tag="w_raw0", align_bytes=64)[:]
+            else:
+                start = S + a * K_PASS
+                raw = held[:, start : start + K_PASS].rearrange("p (j n) -> p j n", j=PACK)
+            nc.sync.dma_start(out=raw, in_=by_partition(w, a))
             w_raw.append(raw)
         bias = keep.tile([P, 1], F32, name="bias")
         nc.sync.dma_start(out=bias[:], in_=b)
@@ -122,19 +127,14 @@ def tile_picked_pick_lin_silu_sub_e_kernel(tc, xT, w, b, offs, out):
                     )
             return window
 
-        picked = {}
-        for a in range(LAST):
-            whole = keep.tile([P, 2, S], U32, name="picked%d" % a, align_bytes=64)
-            picked[a, 0, S] = whole[:]
-            for lo, hi in pieces[a]:
-                picked[a, lo, hi] = whole[:, :, lo:hi]
-        for lo, hi in pieces[LAST]:
-            picked[LAST, lo, hi] = keep.tile([P, 2, hi - lo], U32, name="picked_last%d" % lo, align_bytes=64)[:]
+        picked = [keep.tile([P, 2 * S], U32, name="picked%d" % a, align_bytes=64)[:] for a in range(LAST)]
+        picked.append(held[:, : 2 * S].bitcast(U32))
+        picked = [words.rearrange("p (u n) -> p u n", u=2) for words in picked]
 
         def gather(q, window, lo, hi):
             a, u = divmod(q, 2)
             nc.vector.tensor_copy(
-                picked[a, lo, hi][:, u, :], window[:].indirect(offsets[:, lo // LIST_ROWS : hi // LIST_ROWS])
+                picked[a][:, u, lo:hi], window[:].indirect(offsets[:, lo // LIST_ROWS : hi // LIST_ROWS])
             )
 
         def weave(a, lo, hi):
@@ -145,7 +145,7 @@ def tile_picked_pick_lin_silu_sub_e_kernel(tc, xT, w, b, offs, out):
             else:
                 tag = last_load_of_w if (a, lo) == (LAST, 0) else name
                 woven = keep.tile(shape, U32, name=name, tag=tag, align_bytes=64)
-            src = picked[a, lo, hi].rearrange("p u n -> p n u")
+            src = picked[a][:, :, lo:hi].rearrange("p u n -> p n u")
             if a == 0 and lo > 0:
                 nc.vector.tensor_copy(out=woven[:].bitcast(I32), in_=src.bitcast(I32))
             else:
@@ -165,14 +165,26 @@ def tile_picked_pick_lin_silu_sub_e_kernel(tc, xT, w, b, offs, out):
 
         weights = {}
 
-        def quantize_w(passes, grouped):
+        def quantize_w(passes):
             count = len(passes)
+            grouped = keep.tile([P, count * K_PASS], BF16, name="grouped%d" % passes[0], tag="grouped", align_bytes=64)[:]
             for n, a in enumerate(passes):
-                nc.scalar.activation(
-                    out=grouped[:, n * K_PASS : (n + 1) * K_PASS].rearrange("p (c i j) -> p c j i", i=RUN, j=PACK),
-                    in_=w_raw[a][:].rearrange("p j (c i) -> p c j i", i=RUN),
-                    func=COPY,
-                )
+                dst = grouped[:, n * K_PASS : (n + 1) * K_PASS]
+                if a == 0:
+                    nc.scalar.activation(
+                        out=dst.rearrange("p (c i j) -> p c j i", i=RUN, j=PACK),
+                        in_=w_raw[a].rearrange("p j (c i) -> p c j i", i=RUN),
+                        func=COPY,
+                    )
+                else:
+                    nc.gpsimd.tensor_scalar(
+                        out=dst.rearrange("p (n j) -> p n j", j=PACK),
+                        in0=w_raw[a].rearrange("p j n -> p n j"),
+                        scalar1=1.0,
+                        scalar2=0.0,
+                        op0=MULT,
+                        op1=ADD,
+                    )
             words = keep.tile([P, count * N], U32, name="w_words%d" % passes[0], align_bytes=64)
             scales = keep.tile([P, count * N], U8, name="w_scales%d" % passes[0], align_bytes=64)
             nc.vector.quantize_mx(out=words[:].bitcast(FP8X4), scales=scales[:], in_=grouped)
@@ -196,7 +208,7 @@ def tile_picked_pick_lin_silu_sub_e_kernel(tc, xT, w, b, offs, out):
         for q in range(LAST_PAIR):
             a, u = divmod(q, 2)
             window = round_pair(q)
-            for lo, hi in [(0, S)] if u == 0 and a < LAST else pieces[a]:
+            for lo, hi in [(0, S)] if u == 0 else pieces[a]:
                 gather(q, window, lo, hi)
             if u == 1:
                 woven = [weave(a, lo, hi) for lo, hi in pieces[a]]
@@ -204,15 +216,16 @@ def tile_picked_pick_lin_silu_sub_e_kernel(tc, xT, w, b, offs, out):
                     quantize(a, lo, hi, tile)
 
         window = round_pair(LAST_PAIR)
-        first, second, third = pieces[LAST]
+        first, second, third, fourth = pieces[LAST]
         gather(LAST_PAIR, window, *first)
-        quantize_w(list(range(LAST)), picked[(LAST,) + second][:, 1, :].bitcast(BF16))
+        quantize_w(list(range(LAST)))
         for a in range(LAST):
             for bank, (lo, hi) in zip(banks, out_spans):
                 multiply(a, bank, lo, hi)
         gather(LAST_PAIR, window, *second)
-        quantize_w([LAST], picked[(LAST,) + third][:, 1, :].bitcast(BF16))
         gather(LAST_PAIR, window, *third)
+        quantize_w([LAST])
+        gather(LAST_PAIR, window, *fourth)
         for start, stop in pieces[LAST]:
             quantize(LAST, start, stop, weave(LAST, start, stop))
             for bank, (lo, hi) in zip(banks, out_spans):

@@ -43,7 +43,7 @@ STEPS = (
 EARLY_PIECES = (512, 768)
 LAST_PIECES = (512, 256, 256, 256)
 QUANTIZE_WIDTHS = {256: (256,), 512: (512,), 768: (512, 256)}
-OUT_SLICES = (512, 256, 256, 256)
+OUT_SLICES = (256, 256, 256, 256, 256)
 
 
 def cuts(widths):
@@ -227,9 +227,10 @@ def tile_picked_pick_lin_silu_sub_e_kernel(tc, xT, w, b, offs, out):
         quantize_w([LAST])
         gather(LAST_PAIR, window, *fourth)
         for start, stop in pieces[LAST]:
-            quantize(LAST, start, stop, weave(LAST, start, stop))
+            woven = weave(LAST, start, stop)
             for bank, (lo, hi) in zip(banks, out_spans):
                 if start <= lo < stop:
+                    quantize(LAST, lo, hi, woven[:, lo - start : hi - start, :])
                     multiply(LAST, bank, lo, hi)
                     y = keep.tile([N, hi - lo], F32, name="y%d" % lo)
                     nc.scalar.activation(out=y[:], in_=bank[:], func=SILU, bias=bias[:])

@@ -29,18 +29,16 @@ RUN = 4
 HALF = T // 2
 QUARTER = T // 4
 
-WITH_VECTOR = 352
-WITH_GPSIMD = 576
-WHILE_WEAVING = 416
 STEPS = (
-    ((T, 2 * WITH_VECTOR, "vector"),),
-    ((HALF, WITH_GPSIMD, "gpsimd"), (HALF, WITH_VECTOR, "vector")),
-    ((HALF, WITH_GPSIMD, "gpsimd"), (HALF, HALF, None)),
-    ((HALF, WITH_GPSIMD, "gpsimd"), (HALF, WITH_GPSIMD, "gpsimd")),
-    ((HALF, WITH_GPSIMD, "gpsimd"), (HALF, WITH_VECTOR, "vector")),
-    ((HALF, WHILE_WEAVING, "gpsimd"), (QUARTER, QUARTER // 2, "gpsimd"), (QUARTER, QUARTER, None)),
+    ((T, 704, "vector"),),
+    ((HALF, 640, "gpsimd"), (HALF, 352, "vector")),
+    ((HALF, 640, "gpsimd"), (HALF, 416, "vector")),
+    ((HALF, 640, "gpsimd"), (HALF, 416, "vector")),
+    ((HALF, 640, "gpsimd"), (HALF, 416, "vector")),
+    ((896, 256, "gpsimd"), (768, 384, "gpsimd"), (384, 384, None)),
 )
-EARLY_PIECES = (512, 768)
+EARLY_PIECES = (256, 256, 768)
+EARLY_FIRST = 512
 LAST_PIECES = (512, 256, 256, 256)
 QUANTIZE_WIDTHS = {256: (256,), 512: (512,), 768: (512, 256)}
 OUT_SLICES = (256, 256, 256, 256, 256)
@@ -67,7 +65,7 @@ def tile_picked_pick_lin_silu_sub_e_kernel(tc, xT, w, b, offs, out):
             return rows[a * K_PASS : (a + 1) * K_PASS, :].rearrange("(p j) c -> p j c", j=PACK)
 
         last_load_of_w = "w_raw0"
-        woven_bytes = EARLY_PIECES[1] * PACK * 2
+        woven_bytes = EARLY_PIECES[-1] * PACK * 2
 
         offsets = keep.tile([P, S // LIST_ROWS], U16, name="offsets")
         pair_rows = xT.rearrange("(a p u e) t -> a u p (e t)", p=P, u=2, e=2)
@@ -77,7 +75,7 @@ def tile_picked_pick_lin_silu_sub_e_kernel(tc, xT, w, b, offs, out):
             if q == LAST_PAIR - 1:
                 raw = shared.tile([P, 2 * T], F32, name="x_raw_shared", offset=0, align_bytes=64)
             else:
-                raw = keep.tile([P, 2 * T], F32, name="x_raw%d" % q, align_bytes=64)
+                raw = keep.tile([P, 2 * T], F32, name="x_raw%d" % q, tag="x_raw%d" % q, align_bytes=64)
             start = 0
             for lo, hi in cuts([step[0] for step in STEPS[q]]):
                 nc.sync.dma_start(out=raw[:, start : T + hi], in_=pair_rows[a, u][:, start : T + hi])
@@ -137,22 +135,20 @@ def tile_picked_pick_lin_silu_sub_e_kernel(tc, xT, w, b, offs, out):
                 picked[a][:, u, lo:hi], window[:].indirect(offsets[:, lo // LIST_ROWS : hi // LIST_ROWS])
             )
 
-        def weave(a, lo, hi):
-            shape = [P, hi - lo, 2]
-            name = "woven%d_%d" % (a, lo)
-            if a == LAST - 1 and lo > 0:
+        def weave(a, spans):
+            start, stop = spans[0][0], spans[-1][1]
+            shape = [P, stop - start, 2]
+            name = "woven%d_%d" % (a, start)
+            if a == LAST - 1 and start > 0:
                 woven = shared.tile(shape, U32, name=name, offset=0, align_bytes=64)
             else:
-                tag = last_load_of_w if (a, lo) == (LAST, 0) else name
+                tag = {(LAST, 0): last_load_of_w, (0, EARLY_FIRST): "x_raw2"}.get((a, start), name)
                 woven = keep.tile(shape, U32, name=name, tag=tag, align_bytes=64)
-            src = picked[a][:, :, lo:hi].rearrange("p u n -> p n u")
-            if a == 0 and lo > 0:
-                nc.vector.tensor_copy(out=woven[:].bitcast(I32), in_=src.bitcast(I32))
-            else:
-                nc.scalar.copy(out=woven[:], in_=src)
+            for lo, hi in spans:
+                nc.scalar.copy(out=woven[:, lo - start : hi - start, :], in_=picked[a][:, :, lo:hi].rearrange("p u n -> p n u"))
             return woven
 
-        x_words = [keep.tile([P, S], U32, name="x_words%d" % a, align_bytes=64) for a in range(PASSES)]
+        x_words = [keep.tile([P, S], U32, name="x_words%d" % a, align_bytes=64) for a in range(LAST)]
         x_scales = [keep.tile([P, S], U8, name="x_scales%d" % a, align_bytes=64) for a in range(PASSES)]
 
         def quantize(a, lo, hi, woven):
@@ -211,9 +207,9 @@ def tile_picked_pick_lin_silu_sub_e_kernel(tc, xT, w, b, offs, out):
             for lo, hi in [(0, S)] if u == 0 else pieces[a]:
                 gather(q, window, lo, hi)
             if u == 1:
-                woven = [weave(a, lo, hi) for lo, hi in pieces[a]]
-                for (lo, hi), tile in zip(pieces[a], woven):
-                    quantize(a, lo, hi, tile)
+                quantize(a, 0, EARLY_FIRST, weave(a, pieces[a][:-1]))
+            elif a > 0:
+                quantize(a - 1, EARLY_FIRST, S, weave(a - 1, pieces[a - 1][-1:]))
 
         window = round_pair(LAST_PAIR)
         first, second, third, fourth = pieces[LAST]
@@ -225,9 +221,10 @@ def tile_picked_pick_lin_silu_sub_e_kernel(tc, xT, w, b, offs, out):
         gather(LAST_PAIR, window, *second)
         gather(LAST_PAIR, window, *third)
         quantize_w([LAST])
+        x_words.append(keep.tile([P, S], U32, name="x_words_last", tag="grouped", align_bytes=64))
         gather(LAST_PAIR, window, *fourth)
         for start, stop in pieces[LAST]:
-            woven = weave(LAST, start, stop)
+            woven = weave(LAST, [(start, stop)])
             for bank, (lo, hi) in zip(banks, out_spans):
                 if start <= lo < stop:
                     quantize(LAST, lo, hi, woven[:, lo - start : hi - start, :])

@@ -39,7 +39,7 @@ STEPS = (
 )
 EARLY_PIECES = (256, 256, 768)
 EARLY_FIRST = 512
-LAST_PIECES = (512, 256, 256, 256)
+LAST_PIECES = (256, 256, 256, 256, 256)
 QUANTIZE_WIDTHS = {256: (256,), 512: (512,), 768: (512, 256)}
 OUT_SLICES = (256, 256, 256, 256, 256)
 
@@ -64,7 +64,7 @@ def tile_picked_pick_lin_silu_sub_e_kernel(tc, xT, w, b, offs, out):
         def by_partition(rows, a):
             return rows[a * K_PASS : (a + 1) * K_PASS, :].rearrange("(p j) c -> p j c", j=PACK)
 
-        last_load_of_w = "w_raw0"
+        last_load_of_w = "w_raw1"
         woven_bytes = EARLY_PIECES[-1] * PACK * 2
 
         offsets = keep.tile([P, S // LIST_ROWS], U16, name="offsets")
@@ -87,13 +87,13 @@ def tile_picked_pick_lin_silu_sub_e_kernel(tc, xT, w, b, offs, out):
             raw = keep.tile([P, 2, hi - lo], F32, name="x_last%d" % lo, align_bytes=64)
             nc.sync.dma_start(out=raw[:], in_=by_partition(xT, LAST)[:, 2:, lo:hi])
             x_raw[LAST_PAIR, lo] = raw[:]
-        held = keep.tile([P, S + PASSES * K_PASS], F32, name="held", align_bytes=64)
+        held = keep.tile([P, 2 * S], F32, name="held", align_bytes=64)
         w_raw = []
         for a in range(PASSES):
-            if a == 0:
-                raw = keep.tile([P, PACK, N], F32, name="w_raw0", tag="w_raw0", align_bytes=64)[:]
+            if a == 1:
+                raw = keep.tile([P, PACK, N], F32, name="w_raw1", tag="w_raw1", align_bytes=64)[:]
             else:
-                start = S + a * K_PASS
+                start = S + LAST_PIECES[0] + a // 2 * K_PASS
                 raw = held[:, start : start + K_PASS].rearrange("p (j n) -> p j n", j=PACK)
             nc.sync.dma_start(out=raw, in_=by_partition(w, a))
             w_raw.append(raw)
@@ -161,12 +161,11 @@ def tile_picked_pick_lin_silu_sub_e_kernel(tc, xT, w, b, offs, out):
 
         weights = {}
 
-        def quantize_w(passes):
+        def quantize_w(passes, grouped):
             count = len(passes)
-            grouped = keep.tile([P, count * K_PASS], BF16, name="grouped%d" % passes[0], tag="grouped", align_bytes=64)[:]
             for n, a in enumerate(passes):
                 dst = grouped[:, n * K_PASS : (n + 1) * K_PASS]
-                if a == 0:
+                if a < LAST:
                     nc.scalar.activation(
                         out=dst.rearrange("p (c i j) -> p c j i", i=RUN, j=PACK),
                         in_=w_raw[a].rearrange("p j (c i) -> p c j i", i=RUN),
@@ -212,23 +211,23 @@ def tile_picked_pick_lin_silu_sub_e_kernel(tc, xT, w, b, offs, out):
                 quantize(a - 1, EARLY_FIRST, S, weave(a - 1, pieces[a - 1][-1:]))
 
         window = round_pair(LAST_PAIR)
-        first, second, third, fourth = pieces[LAST]
-        gather(LAST_PAIR, window, *first)
-        quantize_w(list(range(LAST)))
-        for a in range(LAST):
-            for bank, (lo, hi) in zip(banks, out_spans):
-                multiply(a, bank, lo, hi)
-        gather(LAST_PAIR, window, *second)
-        gather(LAST_PAIR, window, *third)
-        quantize_w([LAST])
+        rounded_w = keep.tile([P, 2 * K_PASS], BF16, name="rounded_w", tag="grouped", align_bytes=64)
+        gather(LAST_PAIR, window, *pieces[LAST][0])
+        quantize_w([0], rounded_w[:, K_PASS:])
+        for bank, (lo, hi) in zip(banks, out_spans):
+            multiply(0, bank, lo, hi)
+        for lo, hi in pieces[LAST][1:3]:
+            gather(LAST_PAIR, window, lo, hi)
+        quantize_w([1, LAST], rounded_w[:])
+        for bank, (lo, hi) in zip(banks, out_spans):
+            multiply(1, bank, lo, hi)
+        for lo, hi in pieces[LAST][3:]:
+            gather(LAST_PAIR, window, lo, hi)
         x_words.append(keep.tile([P, S], U32, name="x_words_last", tag="grouped", align_bytes=64))
-        gather(LAST_PAIR, window, *fourth)
-        for start, stop in pieces[LAST]:
-            woven = weave(LAST, [(start, stop)])
-            for bank, (lo, hi) in zip(banks, out_spans):
-                if start <= lo < stop:
-                    quantize(LAST, lo, hi, woven[:, lo - start : hi - start, :])
-                    multiply(LAST, bank, lo, hi)
-                    y = keep.tile([N, hi - lo], F32, name="y%d" % lo)
-                    nc.scalar.activation(out=y[:], in_=bank[:], func=SILU, bias=bias[:])
-                    nc.sync.dma_start(out=out[:, lo:hi], in_=y[:])
+        woven = weave(LAST, pieces[LAST])
+        for bank, (lo, hi) in zip(banks, out_spans):
+            quantize(LAST, lo, hi, woven[:, lo:hi, :])
+            multiply(LAST, bank, lo, hi)
+            y = keep.tile([N, hi - lo], F32, name="y%d" % lo)
+            nc.scalar.activation(out=y[:], in_=bank[:], func=SILU, bias=bias[:])
+            nc.sync.dma_start(out=out[:, lo:hi], in_=y[:])

@@ -40,6 +40,12 @@ STEPS = (
 EARLY_PIECES = (256, 256, 768)
 EARLY_FIRST = 512
 LAST_PIECES = (256, 256, 256, 256, 256)
+BLOCK = 256
+BLOCKS = S // BLOCK
+LAST_AT = (5, 8, 10, 11, 6)
+FIRST_WOVEN_AT = 12
+HELD_BLOCKS = 14
+W_RAW_AT = (8 * BLOCK, 10 * BLOCK + BLOCK // 2, 6 * BLOCK)
 QUANTIZE_WIDTHS = {256: (256,), 512: (512,), 768: (512, 256)}
 OUT_SLICES = (256, 256, 256, 256, 256)
 
@@ -87,14 +93,10 @@ def tile_picked_pick_lin_silu_sub_e_kernel(tc, xT, w, b, offs, out):
             raw = keep.tile([P, 2, hi - lo], F32, name="x_last%d" % lo, align_bytes=64)
             nc.sync.dma_start(out=raw[:], in_=by_partition(xT, LAST)[:, 2:, lo:hi])
             x_raw[LAST_PAIR, lo] = raw[:]
-        held = keep.tile([P, 2 * S], F32, name="held", align_bytes=64)
+        held = keep.tile([P, HELD_BLOCKS * BLOCK], F32, name="held", align_bytes=64)
         w_raw = []
         for a in range(PASSES):
-            if a == 1:
-                raw = keep.tile([P, PACK, N], F32, name="w_raw1", tag="w_raw1", align_bytes=64)[:]
-            else:
-                start = S + LAST_PIECES[0] + a // 2 * K_PASS
-                raw = held[:, start : start + K_PASS].rearrange("p (j n) -> p j n", j=PACK)
+            raw = held[:, W_RAW_AT[a] : W_RAW_AT[a] + K_PASS].rearrange("p (j n) -> p j n", j=PACK)
             nc.sync.dma_start(out=raw, in_=by_partition(w, a))
             w_raw.append(raw)
         bias = keep.tile([P, 1], F32, name="bias")
@@ -211,22 +213,30 @@ def tile_picked_pick_lin_silu_sub_e_kernel(tc, xT, w, b, offs, out):
                 quantize(a - 1, EARLY_FIRST, S, weave(a - 1, pieces[a - 1][-1:]))
 
         window = round_pair(LAST_PAIR)
+        blocks = held[:].bitcast(U32).rearrange("p (b n) -> p b n", n=BLOCK)
+
+        def gather_last(i):
+            columns = BLOCK // LIST_ROWS
+            nc.vector.tensor_copy(blocks[:, LAST_AT[i], :], window[:].indirect(offsets[:, i * columns : (i + 1) * columns]))
+
         rounded_w = keep.tile([P, 2 * K_PASS], BF16, name="rounded_w", tag="grouped", align_bytes=64)
-        gather(LAST_PAIR, window, *pieces[LAST][0])
-        quantize_w([0], rounded_w[:, K_PASS:])
-        for bank, (lo, hi) in zip(banks, out_spans):
-            multiply(0, bank, lo, hi)
-        for lo, hi in pieces[LAST][1:3]:
-            gather(LAST_PAIR, window, lo, hi)
-        quantize_w([1, LAST], rounded_w[:])
-        for bank, (lo, hi) in zip(banks, out_spans):
-            multiply(1, bank, lo, hi)
-        for lo, hi in pieces[LAST][3:]:
-            gather(LAST_PAIR, window, lo, hi)
+        for a, ahead in enumerate(((0,), (1,), (2, 3))):
+            for i in ahead:
+                gather_last(i)
+            quantize_w([a], rounded_w[:, K_PASS:] if a else rounded_w[:, :K_PASS])
+            if a < LAST:
+                for bank, (lo, hi) in zip(banks, out_spans):
+                    multiply(a, bank, lo, hi)
+        gather_last(4)
         x_words.append(keep.tile([P, S], U32, name="x_words_last", tag="grouped", align_bytes=64))
-        woven = weave(LAST, pieces[LAST])
-        for bank, (lo, hi) in zip(banks, out_spans):
-            quantize(LAST, lo, hi, woven[:, lo:hi, :])
+        later = keep.tile([P, S - BLOCK, 2], U32, name="woven_last", align_bytes=64)
+        woven = [blocks[:, FIRST_WOVEN_AT:, :].rearrange("p b (n u) -> p (b n) u", u=2)]
+        woven.extend(later[:, lo:hi, :] for lo, hi in cuts((BLOCK,) * (BLOCKS - 1)))
+        for i in range(BLOCKS):
+            both = blocks[:, i : LAST_AT[i] + 1 : LAST_AT[i] - i, :]
+            nc.scalar.copy(out=woven[i], in_=both.rearrange("p u n -> p n u"))
+        for i, (bank, (lo, hi)) in enumerate(zip(banks, out_spans)):
+            quantize(LAST, lo, hi, woven[i])
             multiply(LAST, bank, lo, hi)
             y = keep.tile([N, hi - lo], F32, name="y%d" % lo)
             nc.scalar.activation(out=y[:], in_=bank[:], func=SILU, bias=bias[:])

from contextlib import ExitStack

import concourse.mybir as mybir

K, T, S, N = 1536, 2048, 1280, 128
FLOPS = 2 * K * S * N

F32 = mybir.dt.float32
BF16 = mybir.dt.bfloat16
I32 = mybir.dt.int32
U32 = mybir.dt.uint32
U16 = mybir.dt.uint16
U8 = mybir.dt.uint8
FP8X4 = mybir.dt.float8_e4m3fn_x4
COPY = mybir.ActivationFunctionType.Copy
SILU = mybir.ActivationFunctionType.Silu
MULT = mybir.AluOpType.mult
ADD = mybir.AluOpType.add

P = 128
PACK = 4
K_PASS = P * PACK
PASSES = K // K_PASS
LAST = PASSES - 1
PAIRS = 2 * PASSES
LAST_PAIR = PAIRS - 1
LIST_ROWS = 16
RUN = 4
HALF = T // 2
QUARTER = T // 4

STEPS = (
    ((T, 704, "vector"),),
    ((HALF, 640, "gpsimd"), (HALF, 352, "vector")),
    ((HALF, 640, "gpsimd"), (HALF, 416, "vector")),
    ((HALF, 640, "gpsimd"), (HALF, 416, "vector")),
    ((HALF, 640, "gpsimd"), (HALF, 416, "vector")),
    ((896, 256, "gpsimd"), (768, 384, "gpsimd"), (384, 384, None)),
)
EARLY_PIECES = (256, 256, 768)
EARLY_FIRST = 512
LAST_PIECES = (256, 256, 256, 256, 256)
BLOCK = 256
BLOCKS = S // BLOCK
LAST_AT = (5, 8, 10, 11, 6)
FIRST_WOVEN_AT = 12
HELD_BLOCKS = 14
W_RAW_AT = (8 * BLOCK, 10 * BLOCK + BLOCK // 2, 6 * BLOCK)
QUANTIZE_WIDTHS = {256: (256,), 512: (512,), 768: (512, 256)}
OUT_SLICES = (256, 256, 256, 256, 256)


def cuts(widths):
    spans = []
    start = 0
    for width in widths:
        spans.append((start, start + width))
        start += width
    return spans


def tile_picked_pick_lin_silu_sub_e_kernel(tc, xT, w, b, offs, out):
    nc = tc.nc
    with ExitStack() as ctx:
        keep = ctx.enter_context(tc.tile_pool(name="keep", bufs=1))
        ring = ctx.enter_context(tc.tile_pool(name="ring", bufs=4))
        shared = ctx.enter_context(tc.tile_pool(name="shared", bufs=1))
        psum = ctx.enter_context(tc.psum_pool(name="psum", bufs=1))

        def by_partition(rows, a):
            return rows[a * K_PASS : (a + 1) * K_PASS, :].rearrange("(p j) c -> p j c", j=PACK)

        last_load_of_w = "w_raw1"
        woven_bytes = EARLY_PIECES[-1] * PACK * 2

        offsets = keep.tile([P, S // LIST_ROWS], U16, name="offsets")
        pair_rows = xT.rearrange("(a p u e) t -> a u p (e t)", p=P, u=2, e=2)
        x_raw = {}
        for q in range(LAST_PAIR):
            a, u = divmod(q, 2)
            if q == LAST_PAIR - 1:
                raw = shared.tile([P, 2 * T], F32, name="x_raw_shared", offset=0, align_bytes=64)
            else:
                raw = keep.tile([P, 2 * T], F32, name="x_raw%d" % q, tag="x_raw%d" % q, align_bytes=64)
            start = 0
            for lo, hi in cuts([step[0] for step in STEPS[q]]):
                nc.sync.dma_start(out=raw[:, start : T + hi], in_=pair_rows[a, u][:, start : T + hi])
                x_raw[q, lo] = raw[:].rearrange("p (e t) -> p e t", e=2)[:, :, lo:hi]
                start = T + hi
            if q == 0:
                nc.sync.dma_start(offsets[:], offs)
        for lo, hi in cuts([step[0] for step in STEPS[LAST_PAIR]]):
            raw = keep.tile([P, 2, hi - lo], F32, name="x_last%d" % lo, align_bytes=64)
            nc.sync.dma_start(out=raw[:], in_=by_partition(xT, LAST)[:, 2:, lo:hi])
            x_raw[LAST_PAIR, lo] = raw[:]
        held = keep.tile([P, HELD_BLOCKS * BLOCK], F32, name="held", align_bytes=64)
        w_raw = []
        for a in range(PASSES):
            raw = held[:, W_RAW_AT[a] : W_RAW_AT[a] + K_PASS].rearrange("p (j n) -> p j n", j=PACK)
            nc.sync.dma_start(out=raw, in_=by_partition(w, a))
            w_raw.append(raw)
        bias = keep.tile([P, 1], F32, name="bias")
        nc.sync.dma_start(out=bias[:], in_=b)

        zero = keep.tile([P, 1], F32, name="zero")
        unused = keep.tile([P, 1], F32, name="unused")
        nc.vector.memset(zero[:], 0.0)
        nc.scalar.activation(out=unused[:], in_=zero[:], func=SILU, bias=zero[:])

        pieces = [cuts(EARLY_PIECES)] * LAST + [cuts(LAST_PIECES)]
        out_spans = cuts(OUT_SLICES)

        def round_pair(q):
            if q == LAST_PAIR:
                window = shared.tile([P, T], U32, name="window_shared", offset=woven_bytes, align_bytes=64)
            else:
                window = ring.tile([P, T], U32, name="window")
            for (lo, hi), (width, share, helper) in zip(cuts([step[0] for step in STEPS[q]]), STEPS[q]):
                dst = window[:, lo:hi].bitcast(BF16).rearrange("p (t j) -> p t j", j=2)
                src = x_raw[q, lo].rearrange("p j t -> p t j")
                nc.scalar.activation(out=dst[:, :share, :], in_=src[:, :share, :], func=COPY)
                if helper == "vector":
                    nc.vector.tensor_copy(out=dst[:, share:, :], in_=src[:, share:, :])
                if helper == "gpsimd":
                    nc.gpsimd.tensor_scalar(
                        out=dst[:, share:, :], in0=src[:, share:, :], scalar1=1.0, scalar2=0.0, op0=MULT, op1=ADD
                    )
            return window

        picked = [keep.tile([P, 2 * S], U32, name="picked%d" % a, align_bytes=64)[:] for a in range(LAST)]
        picked.append(held[:, : 2 * S].bitcast(U32))
        picked = [words.rearrange("p (u n) -> p u n", u=2) for words in picked]

        def gather(q, window, lo, hi):
            a, u = divmod(q, 2)
            nc.vector.tensor_copy(
                picked[a][:, u, lo:hi], window[:].indirect(offsets[:, lo // LIST_ROWS : hi // LIST_ROWS])
            )

        def weave(a, spans):
            start, stop = spans[0][0], spans[-1][1]
            shape = [P, stop - start, 2]
            name = "woven%d_%d" % (a, start)
            if a == LAST - 1 and start > 0:
                woven = shared.tile(shape, U32, name=name, offset=0, align_bytes=64)
            else:
                tag = {(LAST, 0): last_load_of_w, (0, EARLY_FIRST): "x_raw2"}.get((a, start), name)
                woven = keep.tile(shape, U32, name=name, tag=tag, align_bytes=64)
            for lo, hi in spans:
                nc.scalar.copy(out=woven[:, lo - start : hi - start, :], in_=picked[a][:, :, lo:hi].rearrange("p u n -> p n u"))
            return woven

        x_words = [keep.tile([P, S], U32, name="x_words%d" % a, align_bytes=64) for a in range(LAST)]
        x_scales = [keep.tile([P, S], U8, name="x_scales%d" % a, align_bytes=64) for a in range(PASSES)]

        def quantize(a, lo, hi, woven):
            for c0, c1 in cuts(QUANTIZE_WIDTHS[hi - lo]):
                nc.vector.quantize_mx(
                    out=x_words[a][:, lo + c0 : lo + c1].bitcast(FP8X4),
                    scales=x_scales[a][:, lo + c0 : lo + c1],
                    in_=woven[:, c0:c1, :].rearrange("p n u -> p (n u)").bitcast(BF16),
                )

        weights = {}

        def quantize_w(passes, grouped):
            count = len(passes)
            for n, a in enumerate(passes):
                dst = grouped[:, n * K_PASS : (n + 1) * K_PASS]
                if a < LAST:
                    nc.scalar.activation(
                        out=dst.rearrange("p (c i j) -> p c j i", i=RUN, j=PACK),
                        in_=w_raw[a].rearrange("p j (c i) -> p c j i", i=RUN),
                        func=COPY,
                    )
                else:
                    nc.gpsimd.tensor_scalar(
                        out=dst.rearrange("p (n j) -> p n j", j=PACK),
                        in0=w_raw[a].rearrange("p j n -> p n j"),
                        scalar1=1.0,
                        scalar2=0.0,
                        op0=MULT,
                        op1=ADD,
                    )
            words = keep.tile([P, count * N], U32, name="w_words%d" % passes[0], align_bytes=64)
            scales = keep.tile([P, count * N], U8, name="w_scales%d" % passes[0], align_bytes=64)
            nc.vector.quantize_mx(out=words[:].bitcast(FP8X4), scales=scales[:], in_=grouped)
            for n, a in enumerate(passes):
                weights[a] = (words[:, n * N : (n + 1) * N], scales[:, n * N : (n + 1) * N])

        banks = [psum.tile([N, hi - lo], F32, name="bank%d" % lo) for lo, hi in out_spans]

        def multiply(a, bank, lo, hi):
            w_words, w_scales = weights[a]
            nc.tensor.matmul_mx(
                out=bank[:],
                lhsT=w_words.bitcast(FP8X4),
                lhsT_scale=w_scales,
                rhs=x_words[a][:, lo:hi].bitcast(FP8X4),
                rhs_scale=x_scales[a][:, lo:hi],
                start=(a == 0),
                stop=(a == LAST),
            )

        for q in range(LAST_PAIR):
            a, u = divmod(q, 2)
            window = round_pair(q)
            for lo, hi in [(0, S)] if u == 0 else pieces[a]:
                gather(q, window, lo, hi)
            if u == 1:
                quantize(a, 0, EARLY_FIRST, weave(a, pieces[a][:-1]))
            elif a > 0:
                quantize(a - 1, EARLY_FIRST, S, weave(a - 1, pieces[a - 1][-1:]))

        window = round_pair(LAST_PAIR)
        blocks = held[:].bitcast(U32).rearrange("p (b n) -> p b n", n=BLOCK)

        def gather_last(i):
            columns = BLOCK // LIST_ROWS
            nc.vector.tensor_copy(blocks[:, LAST_AT[i], :], window[:].indirect(offsets[:, i * columns : (i + 1) * columns]))

        rounded_w = keep.tile([P, 2 * K_PASS], BF16, name="rounded_w", tag="grouped", align_bytes=64)
        for a, ahead in enumerate(((0,), (1,), (2, 3))):
            for i in ahead:
                gather_last(i)
            quantize_w([a], rounded_w[:, K_PASS:] if a else rounded_w[:, :K_PASS])
            if a < LAST:
                for bank, (lo, hi) in zip(banks, out_spans):
                    multiply(a, bank, lo, hi)
        gather_last(4)
        x_words.append(keep.tile([P, S], U32, name="x_words_last", tag="grouped", align_bytes=64))
        later = keep.tile([P, S - BLOCK, 2], U32, name="woven_last", align_bytes=64)
        woven = [blocks[:, FIRST_WOVEN_AT:, :].rearrange("p b (n u) -> p (b n) u", u=2)]
        woven.extend(later[:, lo:hi, :] for lo, hi in cuts((BLOCK,) * (BLOCKS - 1)))
        for i in range(BLOCKS):
            both = blocks[:, i : LAST_AT[i] + 1 : LAST_AT[i] - i, :]
            nc.scalar.copy(out=woven[i], in_=both.rearrange("p u n -> p n u"))
        for i, (bank, (lo, hi)) in enumerate(zip(banks, out_spans)):
            quantize(LAST, lo, hi, woven[i])
            multiply(LAST, bank, lo, hi)
            y = keep.tile([N, hi - lo], F32, name="y%d" % lo)
            nc.scalar.activation(out=y[:], in_=bank[:], func=SILU, bias=bias[:])
            nc.sync.dma_start(out=out[:, lo:hi], in_=y[:])
